import numpy as np
import ml_dtypes


def mxq(x, axis, fmt="e4m3"):
    dtype, down = {"e4m3": (ml_dtypes.float8_e4m3fn, 7), "e5m2": (ml_dtypes.float8_e5m2, 14)}[fmt]
    v = np.moveaxis(np.asarray(x, np.float32).astype(ml_dtypes.bfloat16).astype(np.float64), axis, -1)
    blocks = v.reshape(v.shape[:-1] + (-1, 32))
    amax = np.abs(blocks).max(-1, keepdims=True)
    byte = np.maximum(np.where(amax > 0, np.frexp(amax)[1] - 1 + 127, 0) - down, 1)
    scale = np.exp2(byte - 127.0)
    codes = (blocks / scale).astype(np.float32).astype(dtype).astype(np.float64)
    return np.moveaxis((codes * scale).reshape(v.shape), -1, axis)


WIDE = False


def mx_kscale(k):
    if not WIDE:
        return np.ones(k)
    levels = np.array([10, -10, 5, -5, 0])
    if k % 512:
        return np.exp2(np.random.permutation(np.resize(levels, k // 32))).repeat(32)
    a = np.empty((k // 512, 16))
    for p in range(k // 512):
        a[p, :8] = np.random.permutation(np.resize(levels, 8))
        for g in range(8):
            far = levels[np.abs(levels - a[p, g]) >= 10]
            a[p, g + 8] = far[np.random.randint(len(far))]
    return np.exp2(a.ravel()).repeat(32)


def f64(x):
    return np.asarray(x).astype(np.float64)


def striped(idx):
    return np.tile(idx.reshape(-1, 16).T, (8, 1)).astype(np.uint16)


def unstriped(offs):
    return offs[:16].T.reshape(-1).astype(np.int64)


E2M1 = np.array([0.0, 0.5, 1.0, 1.5, 2.0, 3.0, 4.0, 6.0, -0.0, -0.5, -1.0, -1.5, -2.0, -3.0, -4.0, -6.0])


def pack_weight(w, fmt):
    k, n = w.shape
    w = f64(np.asarray(w, np.float32).astype(ml_dtypes.bfloat16)).reshape(k // 32, 32, n)
    amax = np.abs(w).max(1)
    if fmt == "e4m3":
        byte = np.frexp(amax)[1] - 1 + 127 - 7
    else:
        mant, ex = np.frexp(amax / 6.0)
        byte = np.where(mant > 0.5, ex, ex - 1) + 127
    byte = np.clip(np.where(amax > 0, byte, 1), 1, 254)
    scaled = (w * np.exp2(127.0 - byte)[:, None, :]).reshape(k, n).astype(np.float32)
    by_word = np.ascontiguousarray(scaled.reshape(k // 512, 128, 4, n).transpose(0, 1, 3, 2))
    if fmt == "e4m3":
        words = by_word.astype(ml_dtypes.float8_e4m3fn).view(np.uint8)
    else:
        c = by_word.astype(ml_dtypes.float4_e2m1fn).view(np.uint8) & 0xF
        words = (c[..., 0::2] | (c[..., 1::2] << 4)).reshape(k // 512, 128, 2 * n)
    return np.ascontiguousarray(words), np.ascontiguousarray(byte.astype(np.uint8).reshape(k // 512, 16, n))


def unpack_weight(words, scales, fmt):
    g, _, n = scales.shape
    words = np.ascontiguousarray(words).reshape(g, 128, n, -1)
    if fmt == "e4m3":
        vals = words.view(ml_dtypes.float8_e4m3fn).astype(np.float64)
    else:
        nib = np.empty((g, 128, n, 4), np.uint8)
        nib[..., 0::2] = words & 0xF
        nib[..., 1::2] = words >> 4
        vals = E2M1[nib]
    vals = vals * np.repeat(np.exp2(scales.astype(np.float64) - 127.0), 8, axis=1)[..., None]
    return vals.transpose(0, 1, 3, 2).reshape(g * 512, n)


def gelu(v):
    return 0.5 * v * (1.0 + np.tanh(np.sqrt(2.0 / np.pi) * (v + 0.044715 * v**3)))


def striped8(idx):
    return np.concatenate([v.reshape(-1, 16).T for v in idx]).astype(np.uint16)


def unstriped8(offs):
    return np.stack([offs[16 * g:16 * g + 16].T.reshape(-1) for g in range(8)]).astype(np.int64)


def runs(v, idx8):
    k = np.arange(v.shape[0])
    return v[k[:, None], idx8[k % 512 // 64]]


def put_heads(h, wgs, idx8, t2):
    r = np.arange(h.shape[0])
    page = np.zeros((h.shape[0], t2))
    page[r[:, None], idx8[r % 512 // 64]] = wgs[r // 4 % 128] * h
    return page


def often(T, S):
    return np.random.permutation(T)[(T * np.random.uniform(0, 1, S) ** 4).astype(np.int64)]


K, H, N, T, S, T2 = 1024, 512, 512, 2048, 1024, 2048

def setup_inputs():
    n = np.random.standard_normal
    s = mx_kscale(K)[:, None]
    u = mx_kscale(H)[:, None]
    d = {}
    d["tab_words"], d["tab_scales"] = pack_weight(n((K, T)) * s, "e4m3")
    d["offs"] = striped8(np.stack([often(T, S) for _ in range(8)]))
    d["wa"] = (n((K, H)) / np.sqrt(K) / s * u.T).astype(np.float32)
    d["wb_words"], d["wb_scales"] = pack_weight(n((K, H)) / np.sqrt(K) / s, "e2m1")
    d["wc_words"], d["wc_scales"] = pack_weight(n((K, H)) / np.sqrt(K) / s * u.T, "e4m3")
    d["wd"] = (0.7 * n((H, N)) / np.sqrt(H) / u).astype(np.float32)
    d["we_words"], d["we_scales"] = pack_weight(0.7 * n((H, N)) / np.sqrt(H) / u, "e2m1")
    d["wf"] = (0.7 * n((H, N)) / np.sqrt(H) / u).astype(np.float32)
    d["wgo"] = np.repeat(np.random.uniform(0.5, 2.0, (8, S)), 16, axis=0).astype(np.float32)
    d["offs2"] = striped8(np.stack([np.random.permutation(T2)[:S] for _ in range(8)]))
    return d

def reference(tab_words, tab_scales, offs, wa, wb_words, wb_scales, wc_words, wc_scales,
              wd, we_words, we_scales, wf, wgo, offs2):
    v = runs(unpack_weight(tab_words, tab_scales, "e4m3"), unstriped8(offs))
    wb = unpack_weight(wb_words, wb_scales, "e2m1")
    wc = unpack_weight(wc_words, wc_scales, "e4m3")
    we = unpack_weight(we_words, we_scales, "e2m1")
    a = mxq(f64(wa), 0, "e4m3").T @ v
    b = wb.T @ v
    c = wc.T @ v
    h = mxq(a * b + c, 0, "e4m3")
    y = (mxq(f64(wd), 0, "e4m3").T @ h) * (we.T @ h)
    y = y + (mxq(f64(wf), 0, "e4m3").T @ h)
    return put_heads(y, f64(wgo), unstriped8(offs2), T2)

@@ -1,0 +1,217 @@
+from contextlib import ExitStack
+
+import concourse.mybir as mybir
+from concourse.masks import make_identity
+
+K, H, N, T, S, T2 = 1024, 512, 512, 2048, 1024, 2048
+FLOPS = 2 * S * (3 * K * H + 3 * H * N)
+
+F32 = mybir.dt.float32
+BF16 = mybir.dt.bfloat16
+I32 = mybir.dt.int32
+U32 = mybir.dt.uint32
+U16 = mybir.dt.uint16
+U8 = mybir.dt.uint8
+FP8X4 = mybir.dt.float8_e4m3fn_x4
+FP4X4 = mybir.dt.float4_e2m1fn_x4
+MULT = mybir.AluOpType.mult
+
+P = 128
+PACK = 4
+K_PASS = P * PACK
+PASSES = K // K_PASS
+TILES = S // P
+GATHER = 256
+PER_COLUMN = 16
+
+
+def interleaved(tile):
+    return tile[:].rearrange("p (c i t) -> p c t i", i=4, t=PACK)
+
+
+def by_rows(tile):
+    return tile[:].rearrange("p t (c i) -> p c t i", i=4)
+
+
+def by_slice(bank):
+    return bank[:].rearrange("j (p t) -> j t p", t=PACK)
+
+
+def tile_list_seat_hand_values_kernel(tc, tab_words, tab_scales, offs, wa, wb_words, wb_scales, wc_words,
+                                                wc_scales, wd, we_words, we_scales, wf, wgo, offs2, out):
+    nc = tc.nc
+    with ExitStack() as ctx:
+        keep = ctx.enter_context(tc.tile_pool(name="keep", bufs=1))
+        ring = ctx.enter_context(tc.tile_pool(name="ring", bufs=2))
+        psum = ctx.enter_context(tc.psum_pool(name="psum", bufs=1))
+
+        gather_list = keep.tile([P, S // PER_COLUMN], U16, name="gather_list")
+        scatter_list = keep.tile([P, S // PER_COLUMN], U16, name="scatter_list")
+        table = [keep.tile([P, T], I32, name=f"table{a}", tag=f"table{a}") for a in range(PASSES)]
+        table_scales = [keep.tile([P, T], U8, name=f"table_scales{a}") for a in range(PASSES)]
+        picked_scales = keep.tile([P, PASSES, S], U8, name="picked_scales")
+        v_scales = keep.tile([P, PASSES, S], U8, name="v_scales", align_bytes=64)
+        raw_a = [keep.tile([P, PACK, H], F32, name=f"raw_a{a}") for a in range(PASSES)]
+        raw_d = keep.tile([P, PACK, N], F32, name="raw_d")
+        raw_f = keep.tile([P, PACK, N], F32, name="raw_f")
+        a_codes = [keep.tile([P, H], U32, name=f"a_codes{a}", align_bytes=64) for a in range(PASSES)]
+        d_codes = keep.tile([P, N], U32, name="d_codes", align_bytes=64)
+        f_codes = keep.tile([P, N], U32, name="f_codes", align_bytes=64)
+        b_codes = keep.tile([P, PASSES, 2 * H], U8, name="b_codes", align_bytes=64)
+        c_codes = keep.tile([P, PASSES, H], I32, name="c_codes", align_bytes=64)
+        e_codes = keep.tile([P, 2 * N], U8, name="e_codes", align_bytes=64)
+        abc_scales = keep.tile([P, PASSES, H], U8, name="abc_scales", align_bytes=64)
+        de_scales = keep.tile([P, N], U8, name="de_scales", align_bytes=64)
+        f_scales = keep.tile([P, N], U8, name="f_scales", align_bytes=64)
+        weights = keep.tile([P, S], F32, name="weights")
+        pages = [keep.tile([P, T2], F32, name=f"page{t}") for t in range(PACK - 1)]
+        identity = keep.tile([P, P], F32, name="identity")
+
+        def load_words(a):
+            nc.sync.dma_start(out=table[a][:], in_=tab_words[a].rearrange("p n t -> p (n t)").bitcast(I32))
+
+        def load_rows(raw, rows):
+            nc.sync.dma_start(out=raw[:], in_=rows.rearrange("(p t) c -> p t c", t=PACK))
+
+        def load_scales(planes, first, scales):
+            for q in range(4):
+                nc.sync.dma_start(out=planes[32 * q + first : 32 * q + first + 4].bitcast(I32),
+                                  in_=scales[:, 4 * q : 4 * q + 4, :].rearrange("a r c -> r a c").bitcast(I32))
+
+        for a in range(PASSES):
+            nc.vector.memset(table_scales[a][:].bitcast(I32), 0)
+            nc.scalar.dma_start(out=table_scales[a][0:P:8, :].bitcast(I32), in_=tab_scales[a].bitcast(I32))
+        nc.sync.dma_start(out=gather_list[:], in_=offs)
+        load_words(0)
+        load_rows(raw_a[0], wa[0:K_PASS, :])
+        load_rows(raw_a[1], wa[K_PASS:K, :])
+        load_scales(abc_scales, 8, wc_scales)
+        load_words(1)
+        load_scales(abc_scales, 0, wb_scales)
+        nc.sync.dma_start(out=c_codes[:], in_=wc_words.rearrange("a p n t -> p a (n t)").bitcast(I32))
+        nc.sync.dma_start(out=b_codes[:].bitcast(I32), in_=wb_words.rearrange("a p n -> p a n").bitcast(I32))
+        nc.sync.dma_start(out=e_codes[:].bitcast(I32), in_=we_words[0].bitcast(I32))
+        load_rows(raw_d, wd)
+        for q in range(4):
+            nc.sync.dma_start(out=de_scales[32 * q : 32 * q + 4, :].bitcast(I32),
+                              in_=we_scales[0, 4 * q : 4 * q + 4, :].bitcast(I32))
+        load_rows(raw_f, wf)
+        nc.sync.dma_start(out=scatter_list[:], in_=offs2)
+        nc.sync.dma_start(out=weights[:], in_=wgo)
+
+        make_identity(nc, identity[:])
+        for t in range(PACK - 1):
+            nc.gpsimd.memset(pages[t][:], 0.0)
+
+        for a in range(PASSES):
+            nc.vector.tensor_copy(out=picked_scales[:, a, :], in_=table_scales[a][:].indirect(gather_list[:]))
+        picked_words = picked_scales[:].rearrange("p a s -> p (a s)").bitcast(I32)
+        v_scale_words = v_scales[:].rearrange("p a s -> p (a s)").bitcast(I32)
+        nc.vector.tensor_copy(out=v_scale_words, in_=picked_words)
+        for r in range(1, 4):
+            nc.gpsimd.dma_start(out=v_scale_words[r:P:32, :], in_=picked_words[8 * r : P : 32, :])
+
+        v_codes = {}
+
+        def gather_words(a, g):
+            v_codes[a, g] = keep.tile([P, GATHER], U32, name=f"v_codes{a}_{g}", align_bytes=64)
+            cols = slice(g * GATHER // PER_COLUMN, (g + 1) * GATHER // PER_COLUMN)
+            nc.vector.tensor_copy(out=v_codes[a, g][:], in_=table[a][:].bitcast(U32).indirect(gather_list[:, cols]))
+
+        def round_weight(copy, raw, tag):
+            rounded = keep.tile([P, PACK * H], BF16, name="rounded", tag=tag, align_bytes=64)
+            copy(out=interleaved(rounded), in_=by_rows(raw))
+            return rounded
+
+        def quantize(codes, scales, rounded):
+            nc.vector.quantize_mx(out=codes.bitcast(FP8X4), scales=scales, in_=rounded[:])
+
+        for g in range(S // GATHER):
+            gather_words(0, g)
+        pages.append(keep.tile([P, T2], F32, name="last_page", tag="table0"))
+        nc.vector.memset(pages[PACK - 1][:], 0.0)
+        gather_words(1, 0)
+        for a in range(PASSES):
+            quantize(a_codes[a][:], abc_scales[4:P, a, :], round_weight(nc.scalar.copy, raw_a[a], f"rounded{a}"))
+        for g in range(1, S // GATHER):
+            gather_words(1, g)
+
+        def product(name, lhs, rhs):
+            bank = psum.tile([P, K_PASS], F32, name=name)
+            for a, ((codes, scales), (w_codes, w_scales)) in enumerate(zip(lhs, rhs)):
+                nc.tensor.matmul_mx(out=bank[:], lhsT=codes, lhsT_scale=scales, rhs=w_codes, rhs_scale=w_scales,
+                                    start=(a == 0), stop=(a == len(lhs) - 1))
+            return bank
+
+        def copied(tag, bank):
+            tile = keep.tile([P, PACK, P], F32, name="copied", tag=tag, align_bytes=64)
+            nc.scalar.copy(out=tile[:], in_=by_slice(bank))
+            return tile
+
+        def times(name, bank, factor):
+            tile = ring.tile([P, PACK, P], F32, name=name)
+            nc.vector.tensor_tensor(out=tile[:], in0=by_slice(bank), in1=factor[:], op=MULT)
+            return tile
+
+        def turned_sum(name, terms):
+            bank = psum.tile([P, PACK, P], F32, name=name)
+            for t in range(PACK):
+                for i, term in enumerate(terms):
+                    nc.tensor.matmul(out=bank[:, t, :], lhsT=term[:, t, :], rhs=identity[:], is_transpose=True,
+                                     start=(i == 0), stop=(i == len(terms) - 1))
+            return bank
+
+        h_terms, h, y_terms = {}, {}, {}
+
+        def features(s):
+            g, first = divmod(s * P, GATHER)
+            v = [(v_codes[a, g][:, first : first + P].bitcast(FP8X4), v_scales[:, a, s * P : (s + 1) * P])
+                 for a in range(PASSES)]
+            c = copied(f"c{s % 2}", product("c_bank", v, [(c_codes[:, a, :].bitcast(FP8X4), abc_scales[8:P, a, :])
+                                                  for a in range(PASSES)]))
+            b = copied(f"b{s % 2}", product("b_bank", v, [(b_codes[:, a, :].bitcast(FP4X4), abc_scales[:, a, :])
+                                                  for a in range(PASSES)]))
+            ab = times("ab", product("a_bank", v, [(a_codes[a][:].bitcast(FP8X4), abc_scales[4:P, a, :])
+                                                   for a in range(PASSES)]), b)
+            h_terms[s] = (c, ab)
+
+        def quantize_features(s):
+            bank = turned_sum("h_bank", h_terms[s])
+            rounded = ring.tile([P, P, PACK], BF16, name="h_rounded", align_bytes=64)
+            nc.scalar.copy(out=rounded[:], in_=bank[:].rearrange("p t j -> p j t"))
+            codes = keep.tile([P, P], U32, name=f"h_codes{s}", align_bytes=64)
+            scales = keep.tile([P, P], U8, name=f"h_scales{s}", align_bytes=64)
+            nc.vector.quantize_mx(out=codes[:].bitcast(FP8X4), scales=scales[:],
+                                  in_=rounded[:].rearrange("p j t -> p (j t)"))
+            h[s] = [(codes[:].bitcast(FP8X4), scales[:])]
+
+        def values(s):
+            e = copied(f"e{s % 2}", product("e_bank", h[s], [(e_codes[:].bitcast(FP4X4), de_scales[:])]))
+            de = times("de", product("d_bank", h[s], [(d_codes[:].bitcast(FP8X4), de_scales[4:P, :])]), e)
+            f = copied(f"f{s % 2}", product("f_bank", h[s], [(f_codes[:].bitcast(FP8X4), f_scales[:])]))
+            y_terms[s] = (f, de)
+
+        y = keep.tile([P, PACK, S], F32, name="y")
+
+        def place_values(s):
+            bank = turned_sum("y_bank", y_terms[s])
+            nc.scalar.copy(out=y[:, :, s * P : (s + 1) * P], in_=bank[:])
+            for t in range(PACK):
+                held = TILES - 1 - t
+                if s < held or s == TILES - 1:
+                    lo, hi = min(s, held) * P, (s + 1) * P
+                    window = pages[t][:].indirect(scatter_list[:, lo // PER_COLUMN : hi // PER_COLUMN])
+                    nc.vector.tensor_tensor(out=window, in0=y[:, t, lo:hi], in1=weights[:, lo:hi], op=MULT)
+                if s == TILES - 1:
+                    nc.sync.dma_start(out=out.rearrange("(p t) c -> p t c", t=PACK)[:, t, :], in_=pages[t][:])
+
+        features(0)
+        features(1)
+        quantize(d_codes[:], de_scales[4:P, :], round_weight(nc.vector.tensor_copy, raw_d, "b0"))
+        quantize(f_codes[:], f_scales[:], round_weight(nc.vector.tensor_copy, raw_f, "b1"))
+        quantize_features(0)
+        for step in range(2, TILES + 3):
+            for stage, s in ((values, step - 2), (quantize_features, step - 1), (features, step),
+                             (place_values, step - 3)):
+                if 0 <= s < TILES:
+                    stage(s)

@@ -73,43 +73,50 @@ def tile_list_seat_hand_values_kernel(tc, tab_words, tab_scales, offs, wa, wb_wo
         def load_rows(raw, rows):
             nc.sync.dma_start(out=raw[:], in_=rows.rearrange("(p t) c -> p t c", t=PACK))
 
-        def load_scales(planes, first, scales):
-            for q in range(4):
+        def load_scales(planes, first, scales, quadrants):
+            for q in quadrants:
                 nc.sync.dma_start(out=planes[32 * q + first : 32 * q + first + 4].bitcast(I32),
                                   in_=scales[:, 4 * q : 4 * q + 4, :].rearrange("a r c -> r a c").bitcast(I32))
 
-        for a in range(PASSES):
-            nc.vector.memset(table_scales[a][:].bitcast(I32), 0)
-            nc.scalar.dma_start(out=table_scales[a][0:P:8, :].bitcast(I32), in_=tab_scales[a].bitcast(I32))
         nc.sync.dma_start(out=gather_list[:], in_=offs)
+        for a in range(PASSES):
+            for j in range(2):
+                rows = tab_scales[a, j:16:2, :].bitcast(I32)
+                nc.sync.dma_start(out=table_scales[a][j:P:2, :].bitcast(I32),
+                                  in_=rows.unsqueeze(1).to_broadcast([8, 8, T // 4]))
         load_words(0)
         load_rows(raw_a[0], wa[0:K_PASS, :])
+        load_scales(abc_scales, 8, wc_scales, range(4))
+        load_scales(abc_scales, 0, wb_scales, range(1))
         load_rows(raw_a[1], wa[K_PASS:K, :])
-        load_scales(abc_scales, 8, wc_scales)
+        load_scales(abc_scales, 0, wb_scales, range(1, 4))
         load_words(1)
-        load_scales(abc_scales, 0, wb_scales)
         nc.sync.dma_start(out=c_codes[:], in_=wc_words.rearrange("a p n t -> p a (n t)").bitcast(I32))
         nc.sync.dma_start(out=b_codes[:].bitcast(I32), in_=wb_words.rearrange("a p n -> p a n").bitcast(I32))
-        nc.sync.dma_start(out=e_codes[:].bitcast(I32), in_=we_words[0].bitcast(I32))
         load_rows(raw_d, wd)
         for q in range(4):
             nc.sync.dma_start(out=de_scales[32 * q : 32 * q + 4, :].bitcast(I32),
                               in_=we_scales[0, 4 * q : 4 * q + 4, :].bitcast(I32))
         load_rows(raw_f, wf)
-        nc.sync.dma_start(out=scatter_list[:], in_=offs2)
+        nc.sync.dma_start(out=e_codes[:].bitcast(I32), in_=we_words[0].bitcast(I32))
         nc.sync.dma_start(out=weights[:], in_=wgo)
+        nc.sync.dma_start(out=scatter_list[:], in_=offs2)
 
         make_identity(nc, identity[:])
-        for t in range(PACK - 1):
-            nc.gpsimd.memset(pages[t][:], 0.0)
+        nc.vector.memset(pages[0][:].bitcast(I32), 0)
+        for t in (1, 2):
+            nc.gpsimd.memset(pages[t][:].bitcast(I32), 0)
+        warm = keep.tile([P, 16], F32, name="warm")
+        nc.vector.memset(warm[:, 0:8], 0.0)
+        nc.scalar.copy(out=warm[:, 8:9], in_=warm[:, 0:1])
 
         for a in range(PASSES):
             nc.vector.tensor_copy(out=picked_scales[:, a, :], in_=table_scales[a][:].indirect(gather_list[:]))
         picked_words = picked_scales[:].rearrange("p a s -> p (a s)").bitcast(I32)
         v_scale_words = v_scales[:].rearrange("p a s -> p (a s)").bitcast(I32)
         nc.vector.tensor_copy(out=v_scale_words, in_=picked_words)
-        for r in range(1, 4):
-            nc.gpsimd.dma_start(out=v_scale_words[r:P:32, :], in_=picked_words[8 * r : P : 32, :])
+        for j in range(2):
+            nc.gpsimd.dma_start(out=v_scale_words[2 + j : P : 32, :], in_=picked_words[16 + j : P : 32, :])
 
         v_codes = {}
 
@@ -128,8 +135,8 @@ def tile_list_seat_hand_values_kernel(tc, tab_words, tab_scales, offs, wa, wb_wo
 
         for g in range(S // GATHER):
             gather_words(0, g)
-        pages.append(keep.tile([P, T2], F32, name="last_page", tag="table0"))
-        nc.vector.memset(pages[PACK - 1][:], 0.0)
+        pages.append(keep.tile([P, T2], F32, name="page3", tag="table0"))
+        nc.vector.memset(pages[3][:].bitcast(I32), 0)
         gather_words(1, 0)
         for a in range(PASSES):
             quantize(a_codes[a][:], abc_scales[4:P, a, :], round_weight(nc.scalar.copy, raw_a[a], f"rounded{a}"))
@@ -211,7 +218,7 @@ def tile_list_seat_hand_values_kernel(tc, tab_words, tab_scales, offs, wa, wb_wo
         quantize(f_codes[:], f_scales[:], round_weight(nc.vector.tensor_copy, raw_f, "b1"))
         quantize_features(0)
         for step in range(2, TILES + 3):
-            for stage, s in ((values, step - 2), (quantize_features, step - 1), (features, step),
+            for stage, s in ((features, step), (values, step - 2), (quantize_features, step - 1),
                              (place_values, step - 3)):
                 if 0 <= s < TILES:
                     stage(s)

@@ -15,6 +15,7 @@ U8 = mybir.dt.uint8
 FP8X4 = mybir.dt.float8_e4m3fn_x4
 FP4X4 = mybir.dt.float4_e2m1fn_x4
 MULT = mybir.AluOpType.mult
+ADD = mybir.AluOpType.add
 
 P = 128
 PACK = 4
@@ -23,18 +24,23 @@ PASSES = K // K_PASS
 TILES = S // P
 GATHER = 256
 PER_COLUMN = 16
+ADDED_ON_VECTOR = 4
 
 
 def interleaved(tile):
-    return tile[:].rearrange("p (c i t) -> p c t i", i=4, t=PACK)
+    return tile.rearrange("p (c i t) -> p c t i", i=4, t=PACK)
 
 
 def by_rows(tile):
-    return tile[:].rearrange("p t (c i) -> p c t i", i=4)
+    return tile.rearrange("p t (c i) -> p c t i", i=4)
 
 
 def by_slice(bank):
     return bank[:].rearrange("j (p t) -> j t p", t=PACK)
+
+
+def by_pair(bank):
+    return bank[:].rearrange("j (p u e) -> j u p e", u=2, e=2)
 
 
 def tile_list_seat_hand_values_kernel(tc, tab_words, tab_scales, offs, wa, wb_words, wb_scales, wc_words,
@@ -48,8 +54,8 @@ def tile_list_seat_hand_values_kernel(tc, tab_words, tab_scales, offs, wa, wb_wo
         gather_list = keep.tile([P, S // PER_COLUMN], U16, name="gather_list")
         scatter_list = keep.tile([P, S // PER_COLUMN], U16, name="scatter_list")
         table = [keep.tile([P, T], I32, name=f"table{a}", tag=f"table{a}") for a in range(PASSES)]
-        table_scales = [keep.tile([P, T], U8, name=f"table_scales{a}") for a in range(PASSES)]
-        picked_scales = keep.tile([P, PASSES, S], U8, name="picked_scales")
+        table_scales = keep.tile([P, T], U8, name="table_scales")
+        picked_scales = keep.tile([P, S], U8, name="picked_scales")
         v_scales = keep.tile([P, PASSES, S], U8, name="v_scales", align_bytes=64)
         raw_a = [keep.tile([P, PACK, H], F32, name=f"raw_a{a}") for a in range(PASSES)]
         raw_d = keep.tile([P, PACK, N], F32, name="raw_d")
@@ -60,11 +66,13 @@ def tile_list_seat_hand_values_kernel(tc, tab_words, tab_scales, offs, wa, wb_wo
         b_codes = keep.tile([P, PASSES, 2 * H], U8, name="b_codes", align_bytes=64)
         c_codes = keep.tile([P, PASSES, H], I32, name="c_codes", align_bytes=64)
         e_codes = keep.tile([P, 2 * N], U8, name="e_codes", align_bytes=64)
-        abc_scales = keep.tile([P, PASSES, H], U8, name="abc_scales", align_bytes=64)
-        de_scales = keep.tile([P, N], U8, name="de_scales", align_bytes=64)
+        bc_scales = keep.tile([P, PASSES, H], U8, name="bc_scales", align_bytes=64)
+        a_scales = keep.tile([P, PASSES, H], U8, name="a_scales", align_bytes=64)
+        d_scales = keep.tile([P, N], U8, name="d_scales", align_bytes=64)
+        e_scales = keep.tile([P, 1, N], U8, name="e_scales", align_bytes=64)
         f_scales = keep.tile([P, N], U8, name="f_scales", align_bytes=64)
         weights = keep.tile([P, S], F32, name="weights")
-        pages = [keep.tile([P, T2], F32, name=f"page{t}") for t in range(PACK - 1)]
+        pages = [keep.tile([P, T2], F32, name=f"page{t}") for t in range(PACK)]
         identity = keep.tile([P, P], F32, name="identity")
 
         def load_words(a):
@@ -73,50 +81,48 @@ def tile_list_seat_hand_values_kernel(tc, tab_words, tab_scales, offs, wa, wb_wo
         def load_rows(raw, rows):
             nc.sync.dma_start(out=raw[:], in_=rows.rearrange("(p t) c -> p t c", t=PACK))
 
-        def load_scales(planes, first, scales, quadrants):
-            for q in quadrants:
-                nc.sync.dma_start(out=planes[32 * q + first : 32 * q + first + 4].bitcast(I32),
-                                  in_=scales[:, 4 * q : 4 * q + 4, :].rearrange("a r c -> r a c").bitcast(I32))
+        def load_scales(planes, first, scales, rows):
+            for r in rows:
+                nc.sync.dma_start(out=planes[first + r : P : 32].bitcast(I32),
+                                  in_=scales[:, r:16:4, :].rearrange("a q c -> q a c").bitcast(I32))
+
+        nc.gpsimd.memset(table_scales[:].bitcast(I32), 0)
+        nc.gpsimd.memset(bc_scales[:].rearrange("p a c -> p (a c)").bitcast(I32), 0)
+        nc.gpsimd.memset(e_scales[:].rearrange("p a c -> p (a c)").bitcast(I32), 0)
+        nc.gpsimd.memset(v_scales[:, 1, :].bitcast(I32), 0)
+        make_identity(nc, identity[:])
+        for page in pages:
+            for half in range(2):
+                nc.gpsimd.memset(page[:, half * T2 // 2 : (half + 1) * T2 // 2].bitcast(I32), 0)
 
         nc.sync.dma_start(out=gather_list[:], in_=offs)
-        for a in range(PASSES):
-            for j in range(2):
-                rows = tab_scales[a, j:16:2, :].bitcast(I32)
-                nc.sync.dma_start(out=table_scales[a][j:P:2, :].bitcast(I32),
-                                  in_=rows.unsqueeze(1).to_broadcast([8, 8, T // 4]))
-        load_words(0)
-        load_rows(raw_a[0], wa[0:K_PASS, :])
-        load_scales(abc_scales, 8, wc_scales, range(4))
-        load_scales(abc_scales, 0, wb_scales, range(1))
-        load_rows(raw_a[1], wa[K_PASS:K, :])
-        load_scales(abc_scales, 0, wb_scales, range(1, 4))
-        load_words(1)
-        nc.sync.dma_start(out=c_codes[:], in_=wc_words.rearrange("a p n t -> p a (n t)").bitcast(I32))
-        nc.sync.dma_start(out=b_codes[:].bitcast(I32), in_=wb_words.rearrange("a p n -> p a n").bitcast(I32))
-        load_rows(raw_d, wd)
-        for q in range(4):
-            nc.sync.dma_start(out=de_scales[32 * q : 32 * q + 4, :].bitcast(I32),
-                              in_=we_scales[0, 4 * q : 4 * q + 4, :].bitcast(I32))
-        load_rows(raw_f, wf)
-        nc.sync.dma_start(out=e_codes[:].bitcast(I32), in_=we_words[0].bitcast(I32))
-        nc.sync.dma_start(out=weights[:], in_=wgo)
         nc.sync.dma_start(out=scatter_list[:], in_=offs2)
-
-        make_identity(nc, identity[:])
-        nc.vector.memset(pages[0][:].bitcast(I32), 0)
-        for t in (1, 2):
-            nc.gpsimd.memset(pages[t][:].bitcast(I32), 0)
-        warm = keep.tile([P, 16], F32, name="warm")
-        nc.vector.memset(warm[:, 0:8], 0.0)
-        nc.scalar.copy(out=warm[:, 8:9], in_=warm[:, 0:1])
-
-        for a in range(PASSES):
-            nc.vector.tensor_copy(out=picked_scales[:, a, :], in_=table_scales[a][:].indirect(gather_list[:]))
-        picked_words = picked_scales[:].rearrange("p a s -> p (a s)").bitcast(I32)
-        v_scale_words = v_scales[:].rearrange("p a s -> p (a s)").bitcast(I32)
-        nc.vector.tensor_copy(out=v_scale_words, in_=picked_words)
+        nc.sync.dma_start(out=e_codes[:].bitcast(I32), in_=we_words[0].bitcast(I32))
+        nc.sync.dma_start(out=b_codes[:].bitcast(I32), in_=wb_words.rearrange("a p n -> p a n").bitcast(I32))
         for j in range(2):
-            nc.gpsimd.dma_start(out=v_scale_words[2 + j : P : 32, :], in_=picked_words[16 + j : P : 32, :])
+            nc.sync.dma_start(out=table_scales[j:P:8, :].bitcast(I32),
+                              in_=tab_scales[:, j:16:2, :].rearrange("a g c -> g a c").bitcast(I32))
+        load_words(0)
+        load_scales(bc_scales, 0, wb_scales, range(4))
+        load_scales(e_scales, 0, we_scales, range(2))
+        load_words(1)
+        load_scales(bc_scales, 8, wc_scales, range(4))
+        load_scales(e_scales, 0, we_scales, range(2, 4))
+        load_rows(raw_a[0], wa[0:K_PASS, :])
+
+        nc.vector.tensor_copy(out=picked_scales[:], in_=table_scales[:].indirect(gather_list[:]))
+        picked_words = picked_scales[:].bitcast(I32)
+        nc.vector.tensor_copy(out=v_scales[:, 0, :].bitcast(I32), in_=picked_words)
+        for a, odd in ((0, 1), (1, 0), (1, 1)):
+            for j in range(2):
+                nc.sync.dma_start(out=v_scales[2 * odd + j : P : 32, a, :].bitcast(I32),
+                                  in_=picked_words[16 * odd + 8 * a + j : P : 32, :])
+
+        load_rows(raw_a[1], wa[K_PASS:K, :])
+        nc.sync.dma_start(out=c_codes[:], in_=wc_words.rearrange("a p n t -> p a (n t)").bitcast(I32))
+        load_rows(raw_d, wd)
+        load_rows(raw_f, wf)
+        nc.sync.dma_start(out=weights[:], in_=wgo)
 
         v_codes = {}
 
@@ -125,44 +131,47 @@ def tile_list_seat_hand_values_kernel(tc, tab_words, tab_scales, offs, wa, wb_wo
             cols = slice(g * GATHER // PER_COLUMN, (g + 1) * GATHER // PER_COLUMN)
             nc.vector.tensor_copy(out=v_codes[a, g][:], in_=table[a][:].bitcast(U32).indirect(gather_list[:, cols]))
 
-        def round_weight(copy, raw, tag):
-            rounded = keep.tile([P, PACK * H], BF16, name="rounded", tag=tag, align_bytes=64)
-            copy(out=interleaved(rounded), in_=by_rows(raw))
-            return rounded
-
-        def quantize(codes, scales, rounded):
-            nc.vector.quantize_mx(out=codes.bitcast(FP8X4), scales=scales, in_=rounded[:])
+        def quantize_weight(raw, codes, scales, copies):
+            width = H // len(copies)
+            rounded = []
+            for i, (copy, tag) in enumerate(copies):
+                tile = keep.tile([P, PACK * width], BF16, name="rounded", tag=tag, align_bytes=64)
+                copy(out=interleaved(tile[:]), in_=by_rows(raw[:, :, i * width : (i + 1) * width]))
+                rounded.append(tile)
+            for i, tile in enumerate(rounded):
+                cols = slice(i * width, (i + 1) * width)
+                nc.vector.quantize_mx(out=codes[:, cols].bitcast(FP8X4), scales=scales[:, cols], in_=tile[:])
 
         for g in range(S // GATHER):
-            gather_words(0, g)
-        pages.append(keep.tile([P, T2], F32, name="page3", tag="table0"))
-        nc.vector.memset(pages[3][:].bitcast(I32), 0)
-        gather_words(1, 0)
-        for a in range(PASSES):
-            quantize(a_codes[a][:], abc_scales[4:P, a, :], round_weight(nc.scalar.copy, raw_a[a], f"rounded{a}"))
-        for g in range(1, S // GATHER):
-            gather_words(1, g)
+            for a in range(PASSES):
+                gather_words(a, g)
+        quantize_weight(raw_a[0], a_codes[0], a_scales[:, 0, :], [(nc.scalar.copy, "rounded_a0")])
+        quantize_weight(raw_a[1], a_codes[1], a_scales[:, 1, :],
+                        [(nc.vector.tensor_copy, "rounded_a1"), (nc.scalar.copy, "rounded_a2")])
 
-        def product(name, lhs, rhs):
-            bank = psum.tile([P, K_PASS], F32, name=name)
+        turns = {"first": [], "second": [], "third": []}
+
+        def product(kind, lhs, rhs):
+            bank = psum.tile([P, K_PASS], F32, name="bank", tag=f"{kind}{len(turns[kind]) % 2}")
+            turns[kind].append(bank)
             for a, ((codes, scales), (w_codes, w_scales)) in enumerate(zip(lhs, rhs)):
                 nc.tensor.matmul_mx(out=bank[:], lhsT=codes, lhsT_scale=scales, rhs=w_codes, rhs_scale=w_scales,
                                     start=(a == 0), stop=(a == len(lhs) - 1))
             return bank
 
-        def copied(tag, bank):
-            tile = keep.tile([P, PACK, P], F32, name="copied", tag=tag, align_bytes=64)
-            nc.scalar.copy(out=tile[:], in_=by_slice(bank))
+        def copied(tag, view):
+            tile = keep.tile(view.shape, F32, name="copied", tag=tag, align_bytes=64)
+            nc.scalar.copy(out=tile[:], in_=view)
             return tile
 
-        def times(name, bank, factor):
-            tile = ring.tile([P, PACK, P], F32, name=name)
-            nc.vector.tensor_tensor(out=tile[:], in0=by_slice(bank), in1=factor[:], op=MULT)
+        def times(tag, view, factor):
+            tile = keep.tile(view.shape, F32, name="times", tag=tag, align_bytes=64)
+            nc.vector.tensor_tensor(out=tile[:], in0=view, in1=factor[:], op=MULT)
             return tile
 
         def turned_sum(name, terms):
             bank = psum.tile([P, PACK, P], F32, name=name)
-            for t in range(PACK):
+            for t in range(terms[0].shape[1]):
                 for i, term in enumerate(terms):
                     nc.tensor.matmul(out=bank[:, t, :], lhsT=term[:, t, :], rhs=identity[:], is_transpose=True,
                                      start=(i == 0), stop=(i == len(terms) - 1))
@@ -174,29 +183,39 @@ def tile_list_seat_hand_values_kernel(tc, tab_words, tab_scales, offs, wa, wb_wo
             g, first = divmod(s * P, GATHER)
             v = [(v_codes[a, g][:, first : first + P].bitcast(FP8X4), v_scales[:, a, s * P : (s + 1) * P])
                  for a in range(PASSES)]
-            c = copied(f"c{s % 2}", product("c_bank", v, [(c_codes[:, a, :].bitcast(FP8X4), abc_scales[8:P, a, :])
-                                                  for a in range(PASSES)]))
-            b = copied(f"b{s % 2}", product("b_bank", v, [(b_codes[:, a, :].bitcast(FP4X4), abc_scales[:, a, :])
-                                                  for a in range(PASSES)]))
-            ab = times("ab", product("a_bank", v, [(a_codes[a][:].bitcast(FP8X4), abc_scales[4:P, a, :])
-                                                   for a in range(PASSES)]), b)
-            h_terms[s] = (c, ab)
+            order = by_pair if s < ADDED_ON_VECTOR else by_slice
+            b_bank = product("first", v, [(b_codes[:, a, :].bitcast(FP4X4), bc_scales[:, a, :]) for a in range(PASSES)])
+            b = copied(f"b{s % 3}", order(b_bank))
+            a_bank = product("second", v, [(a_codes[a][:].bitcast(FP8X4), a_scales[:, a, :]) for a in range(PASSES)])
+            ab = times(f"ab{s % 2}", order(a_bank), b)
+            c_bank = product("third", v, [(c_codes[:, a, :].bitcast(FP8X4), bc_scales[8:P, a, :])
+                                           for a in range(PASSES)])
+            if s < ADDED_ON_VECTOR:
+                pairs = keep.tile([P, 2, P, 2], BF16, name="pairs", tag=f"pairs{s % 2}", align_bytes=64)
+                nc.vector.tensor_tensor(out=pairs[:], in0=order(c_bank), in1=ab[:], op=ADD)
+                h_terms[s] = [pairs[:].rearrange("j u p e -> j (u p e)").bitcast(F32).rearrange("j (u p) -> j u p", u=2)]
+            else:
+                h_terms[s] = [copied(f"c{s % 2}", order(c_bank))[:], ab[:]]
 
         def quantize_features(s):
             bank = turned_sum("h_bank", h_terms[s])
-            rounded = ring.tile([P, P, PACK], BF16, name="h_rounded", align_bytes=64)
-            nc.scalar.copy(out=rounded[:], in_=bank[:].rearrange("p t j -> p j t"))
-            codes = keep.tile([P, P], U32, name=f"h_codes{s}", align_bytes=64)
+            rounded = ring.tile([P, P * PACK], BF16, name="h_rounded", align_bytes=64)
+            if s < ADDED_ON_VECTOR:
+                nc.scalar.copy(out=rounded[:].bitcast(F32).rearrange("p (j u) -> p j u", u=2),
+                               in_=bank[:, 0:2, :].rearrange("p u j -> p j u"))
+            else:
+                nc.scalar.copy(out=rounded[:].rearrange("p (j t) -> p j t", t=PACK),
+                               in_=bank[:].rearrange("p t j -> p j t"))
+            codes = keep.tile([P, P], U32, name="h_codes", tag=f"h_codes{s}", align_bytes=64)
             scales = keep.tile([P, P], U8, name=f"h_scales{s}", align_bytes=64)
-            nc.vector.quantize_mx(out=codes[:].bitcast(FP8X4), scales=scales[:],
-                                  in_=rounded[:].rearrange("p j t -> p (j t)"))
+            nc.vector.quantize_mx(out=codes[:].bitcast(FP8X4), scales=scales[:], in_=rounded[:])
             h[s] = [(codes[:].bitcast(FP8X4), scales[:])]
 
         def values(s):
-            e = copied(f"e{s % 2}", product("e_bank", h[s], [(e_codes[:].bitcast(FP4X4), de_scales[:])]))
-            de = times("de", product("d_bank", h[s], [(d_codes[:].bitcast(FP8X4), de_scales[4:P, :])]), e)
-            f = copied(f"f{s % 2}", product("f_bank", h[s], [(f_codes[:].bitcast(FP8X4), f_scales[:])]))
-            y_terms[s] = (f, de)
+            e = copied(f"e{s % 2}", by_slice(product("first", h[s], [(e_codes[:].bitcast(FP4X4), e_scales[:, 0, :])])))
+            de = times(f"de{s % 3}", by_slice(product("second", h[s], [(d_codes[:].bitcast(FP8X4), d_scales[:])])), e)
+            f = copied(f"f{s % 3}", by_slice(product("third", h[s], [(f_codes[:].bitcast(FP8X4), f_scales[:])])))
+            y_terms[s] = [f[:], de[:]]
 
         y = keep.tile([P, PACK, S], F32, name="y")
 
@@ -212,13 +231,14 @@ def tile_list_seat_hand_values_kernel(tc, tab_words, tab_scales, offs, wa, wb_wo
                 if s == TILES - 1:
                     nc.sync.dma_start(out=out.rearrange("(p t) c -> p t c", t=PACK)[:, t, :], in_=pages[t][:])
 
-        features(0)
-        features(1)
-        quantize(d_codes[:], de_scales[4:P, :], round_weight(nc.vector.tensor_copy, raw_d, "b0"))
-        quantize(f_codes[:], f_scales[:], round_weight(nc.vector.tensor_copy, raw_f, "b1"))
-        quantize_features(0)
-        for step in range(2, TILES + 3):
-            for stage, s in ((features, step), (values, step - 2), (quantize_features, step - 1),
-                             (place_values, step - 3)):
-                if 0 <= s < TILES:
+        for stage, s in ((features, 0), (features, 1), (quantize_features, 0)):
+            stage(s)
+        quantize_weight(raw_d, d_codes, d_scales[:], [(nc.scalar.copy, "rounded_d0"), (nc.scalar.copy, "rounded_d1")])
+        quantize_weight(raw_f, f_codes, f_scales[:], [(nc.vector.tensor_copy, "ab1"), (nc.scalar.copy, "rounded_f1")])
+        for stage, s in ((values, 0), (features, 2), (quantize_features, 1), (values, 1), (place_values, 0),
+                         (features, 3), (quantize_features, 2)):
+            stage(s)
+        for j in range(1, TILES):
+            for stage, s in ((values, j + 1), (features, j + 3), (quantize_features, j + 2), (place_values, j)):
+                if s < TILES:
                     stage(s)

@@ -24,7 +24,8 @@ PASSES = K // K_PASS
 TILES = S // P
 GATHER = 256
 PER_COLUMN = 16
-ADDED_ON_VECTOR = 4
+ADDED_ON_VECTOR = 8
+HELD = 6
 
 
 def interleaved(tile):
@@ -223,7 +224,7 @@ def tile_list_seat_hand_values_kernel(tc, tab_words, tab_scales, offs, wa, wb_wo
             bank = turned_sum("y_bank", y_terms[s])
             nc.scalar.copy(out=y[:, :, s * P : (s + 1) * P], in_=bank[:])
             for t in range(PACK):
-                held = TILES - 1 - t
+                held = TILES - (HELD if t == PACK - 1 else 1)
                 if s < held or s == TILES - 1:
                     lo, hi = min(s, held) * P, (s + 1) * P
                     window = pages[t][:].indirect(scatter_list[:, lo // PER_COLUMN : hi // PER_COLUMN])

@@ -24,7 +24,6 @@ PASSES = K // K_PASS
 TILES = S // P
 GATHER = 256
 PER_COLUMN = 16
-ADDED_ON_VECTOR = 8
 HELD = 6
 
 
@@ -103,13 +102,13 @@ def tile_list_seat_hand_values_kernel(tc, tab_words, tab_scales, offs, wa, wb_wo
         for j in range(2):
             nc.sync.dma_start(out=table_scales[j:P:8, :].bitcast(I32),
                               in_=tab_scales[:, j:16:2, :].rearrange("a g c -> g a c").bitcast(I32))
-        load_words(0)
+        load_rows(raw_a[0], wa[0:K_PASS, :])
         load_scales(bc_scales, 0, wb_scales, range(4))
         load_scales(e_scales, 0, we_scales, range(2))
-        load_words(1)
+        load_rows(raw_a[1], wa[K_PASS:K, :])
         load_scales(bc_scales, 8, wc_scales, range(4))
         load_scales(e_scales, 0, we_scales, range(2, 4))
-        load_rows(raw_a[0], wa[0:K_PASS, :])
+        load_words(0)
 
         nc.vector.tensor_copy(out=picked_scales[:], in_=table_scales[:].indirect(gather_list[:]))
         picked_words = picked_scales[:].bitcast(I32)
@@ -119,7 +118,7 @@ def tile_list_seat_hand_values_kernel(tc, tab_words, tab_scales, offs, wa, wb_wo
                 nc.sync.dma_start(out=v_scales[2 * odd + j : P : 32, a, :].bitcast(I32),
                                   in_=picked_words[16 * odd + 8 * a + j : P : 32, :])
 
-        load_rows(raw_a[1], wa[K_PASS:K, :])
+        load_words(1)
         nc.sync.dma_start(out=c_codes[:], in_=wc_words.rearrange("a p n t -> p a (n t)").bitcast(I32))
         load_rows(raw_d, wd)
         load_rows(raw_f, wf)
@@ -143,12 +142,11 @@ def tile_list_seat_hand_values_kernel(tc, tab_words, tab_scales, offs, wa, wb_wo
                 cols = slice(i * width, (i + 1) * width)
                 nc.vector.quantize_mx(out=codes[:, cols].bitcast(FP8X4), scales=scales[:, cols], in_=tile[:])
 
+        for a in range(PASSES):
+            quantize_weight(raw_a[a], a_codes[a], a_scales[:, a, :], [(nc.scalar.copy, f"rounded_a{a}")])
         for g in range(S // GATHER):
             for a in range(PASSES):
                 gather_words(a, g)
-        quantize_weight(raw_a[0], a_codes[0], a_scales[:, 0, :], [(nc.scalar.copy, "rounded_a0")])
-        quantize_weight(raw_a[1], a_codes[1], a_scales[:, 1, :],
-                        [(nc.vector.tensor_copy, "rounded_a1"), (nc.scalar.copy, "rounded_a2")])
 
         turns = {"first": [], "second": [], "third": []}
 
@@ -180,33 +178,37 @@ def tile_list_seat_hand_values_kernel(tc, tab_words, tab_scales, offs, wa, wb_wo
 
         h_terms, h, y_terms = {}, {}, {}
 
-        def features(s):
+        def picked(s):
             g, first = divmod(s * P, GATHER)
-            v = [(v_codes[a, g][:, first : first + P].bitcast(FP8X4), v_scales[:, a, s * P : (s + 1) * P])
-                 for a in range(PASSES)]
-            order = by_pair if s < ADDED_ON_VECTOR else by_slice
-            b_bank = product("first", v, [(b_codes[:, a, :].bitcast(FP4X4), bc_scales[:, a, :]) for a in range(PASSES)])
-            b = copied(f"b{s % 3}", order(b_bank))
-            a_bank = product("second", v, [(a_codes[a][:].bitcast(FP8X4), a_scales[:, a, :]) for a in range(PASSES)])
-            ab = times(f"ab{s % 2}", order(a_bank), b)
-            c_bank = product("third", v, [(c_codes[:, a, :].bitcast(FP8X4), bc_scales[8:P, a, :])
-                                           for a in range(PASSES)])
-            if s < ADDED_ON_VECTOR:
-                pairs = keep.tile([P, 2, P, 2], BF16, name="pairs", tag=f"pairs{s % 2}", align_bytes=64)
-                nc.vector.tensor_tensor(out=pairs[:], in0=order(c_bank), in1=ab[:], op=ADD)
-                h_terms[s] = [pairs[:].rearrange("j u p e -> j (u p e)").bitcast(F32).rearrange("j (u p) -> j u p", u=2)]
-            else:
-                h_terms[s] = [copied(f"c{s % 2}", order(c_bank))[:], ab[:]]
+            return [(v_codes[a, g][:, first : first + P].bitcast(FP8X4), v_scales[:, a, s * P : (s + 1) * P])
+                    for a in range(PASSES)]
+
+        ab = {}
+
+        def feature_product(s):
+            b_bank = product("first", picked(s), [(b_codes[:, a, :].bitcast(FP4X4), bc_scales[:, a, :])
+                                                  for a in range(PASSES)])
+            b = copied(f"b{s % 3}", by_pair(b_bank))
+            a_bank = product("second", picked(s), [(a_codes[a][:].bitcast(FP8X4), a_scales[:, a, :])
+                                                   for a in range(PASSES)])
+            ab[s] = times(f"ab{s % 2}", by_pair(a_bank), b)
+
+        def feature_sum(s):
+            c_bank = product("third", picked(s), [(c_codes[:, a, :].bitcast(FP8X4), bc_scales[8:P, a, :])
+                                                  for a in range(PASSES)])
+            pairs = keep.tile([P, 2, P, 2], BF16, name="pairs", tag=f"pairs{s % 2}", align_bytes=64)
+            nc.vector.tensor_tensor(out=pairs[:], in0=by_pair(c_bank), in1=ab[s][:], op=ADD)
+            h_terms[s] = [pairs[:].rearrange("j u p e -> j (u p e)").bitcast(F32).rearrange("j (u p) -> j u p", u=2)]
+
+        def features(s):
+            feature_product(s)
+            feature_sum(s)
 
         def quantize_features(s):
             bank = turned_sum("h_bank", h_terms[s])
             rounded = ring.tile([P, P * PACK], BF16, name="h_rounded", align_bytes=64)
-            if s < ADDED_ON_VECTOR:
-                nc.scalar.copy(out=rounded[:].bitcast(F32).rearrange("p (j u) -> p j u", u=2),
-                               in_=bank[:, 0:2, :].rearrange("p u j -> p j u"))
-            else:
-                nc.scalar.copy(out=rounded[:].rearrange("p (j t) -> p j t", t=PACK),
-                               in_=bank[:].rearrange("p t j -> p j t"))
+            nc.scalar.copy(out=rounded[:].bitcast(F32).rearrange("p (j u) -> p j u", u=2),
+                           in_=bank[:, 0:2, :].rearrange("p u j -> p j u"))
             codes = keep.tile([P, P], U32, name="h_codes", tag=f"h_codes{s}", align_bytes=64)
             scales = keep.tile([P, P], U8, name=f"h_scales{s}", align_bytes=64)
             nc.vector.quantize_mx(out=codes[:].bitcast(FP8X4), scales=scales[:], in_=rounded[:])
@@ -236,10 +238,11 @@ def tile_list_seat_hand_values_kernel(tc, tab_words, tab_scales, offs, wa, wb_wo
             stage(s)
         quantize_weight(raw_d, d_codes, d_scales[:], [(nc.scalar.copy, "rounded_d0"), (nc.scalar.copy, "rounded_d1")])
         quantize_weight(raw_f, f_codes, f_scales[:], [(nc.vector.tensor_copy, "ab1"), (nc.scalar.copy, "rounded_f1")])
-        for stage, s in ((values, 0), (features, 2), (quantize_features, 1), (values, 1), (place_values, 0),
+        for stage, s in ((values, 0), (place_values, 0), (features, 2), (quantize_features, 1), (values, 1),
                          (features, 3), (quantize_features, 2)):
             stage(s)
         for j in range(1, TILES):
-            for stage, s in ((values, j + 1), (features, j + 3), (quantize_features, j + 2), (place_values, j)):
+            for stage, s in ((feature_product, j + 3), (values, j + 1), (feature_sum, j + 3),
+                             (quantize_features, j + 2), (place_values, j)):
                 if s < TILES:
                     stage(s)

@@ -24,7 +24,10 @@ PASSES = K // K_PASS
 TILES = S // P
 GATHER = 256
 PER_COLUMN = 16
+WC_ROW = 8
+LEAD = 3
 HELD = 6
+ADDED_ON_VECTOR = 5
 
 
 def interleaved(tile):
@@ -44,7 +47,7 @@ def by_pair(bank):
 
 
 def tile_list_seat_hand_values_kernel(tc, tab_words, tab_scales, offs, wa, wb_words, wb_scales, wc_words,
-                                                wc_scales, wd, we_words, we_scales, wf, wgo, offs2, out):
+                                                   wc_scales, wd, we_words, we_scales, wf, wgo, offs2, out):
     nc = tc.nc
     with ExitStack() as ctx:
         keep = ctx.enter_context(tc.tile_pool(name="keep", bufs=1))
@@ -53,14 +56,14 @@ def tile_list_seat_hand_values_kernel(tc, tab_words, tab_scales, offs, wa, wb_wo
 
         gather_list = keep.tile([P, S // PER_COLUMN], U16, name="gather_list")
         scatter_list = keep.tile([P, S // PER_COLUMN], U16, name="scatter_list")
-        table = [keep.tile([P, T], I32, name=f"table{a}", tag=f"table{a}") for a in range(PASSES)]
+        table = [keep.tile([P, T], I32, name=f"table{m}") for m in range(PASSES)]
         table_scales = keep.tile([P, T], U8, name="table_scales")
         picked_scales = keep.tile([P, S], U8, name="picked_scales")
         v_scales = keep.tile([P, PASSES, S], U8, name="v_scales", align_bytes=64)
-        raw_a = [keep.tile([P, PACK, H], F32, name=f"raw_a{a}") for a in range(PASSES)]
+        raw_a = [keep.tile([P, PACK, H], F32, name=f"raw_a{m}") for m in range(PASSES)]
         raw_d = keep.tile([P, PACK, N], F32, name="raw_d")
         raw_f = keep.tile([P, PACK, N], F32, name="raw_f")
-        a_codes = [keep.tile([P, H], U32, name=f"a_codes{a}", align_bytes=64) for a in range(PASSES)]
+        a_codes = [keep.tile([P, H], U32, name=f"a_codes{m}", align_bytes=64) for m in range(PASSES)]
         d_codes = keep.tile([P, N], U32, name="d_codes", align_bytes=64)
         f_codes = keep.tile([P, N], U32, name="f_codes", align_bytes=64)
         b_codes = keep.tile([P, PASSES, 2 * H], U8, name="b_codes", align_bytes=64)
@@ -75,20 +78,20 @@ def tile_list_seat_hand_values_kernel(tc, tab_words, tab_scales, offs, wa, wb_wo
         pages = [keep.tile([P, T2], F32, name=f"page{t}") for t in range(PACK)]
         identity = keep.tile([P, P], F32, name="identity")
 
-        def load_words(a):
-            nc.sync.dma_start(out=table[a][:], in_=tab_words[a].rearrange("p n t -> p (n t)").bitcast(I32))
+        def load_words(m):
+            nc.sync.dma_start(out=table[m][:], in_=tab_words[m].rearrange("p n t -> p (n t)").bitcast(I32))
 
         def load_rows(raw, rows):
             nc.sync.dma_start(out=raw[:], in_=rows.rearrange("(p t) c -> p t c", t=PACK))
 
-        def load_scales(planes, first, scales, rows):
+        def load_scales(tile, first, scales, rows):
             for r in rows:
-                nc.sync.dma_start(out=planes[first + r : P : 32].bitcast(I32),
-                                  in_=scales[:, r:16:4, :].rearrange("a q c -> q a c").bitcast(I32))
+                nc.sync.dma_start(out=tile[first + r : P : 32].bitcast(I32),
+                                  in_=scales[:, r:16:4, :].rearrange("m q c -> q m c").bitcast(I32))
 
         nc.gpsimd.memset(table_scales[:].bitcast(I32), 0)
-        nc.gpsimd.memset(bc_scales[:].rearrange("p a c -> p (a c)").bitcast(I32), 0)
-        nc.gpsimd.memset(e_scales[:].rearrange("p a c -> p (a c)").bitcast(I32), 0)
+        nc.gpsimd.memset(bc_scales[:].rearrange("p m c -> p (m c)").bitcast(I32), 0)
+        nc.gpsimd.memset(e_scales[:].rearrange("p m c -> p (m c)").bitcast(I32), 0)
         nc.gpsimd.memset(v_scales[:, 1, :].bitcast(I32), 0)
         make_identity(nc, identity[:])
         for page in pages:
@@ -98,43 +101,43 @@ def tile_list_seat_hand_values_kernel(tc, tab_words, tab_scales, offs, wa, wb_wo
         nc.sync.dma_start(out=gather_list[:], in_=offs)
         nc.sync.dma_start(out=scatter_list[:], in_=offs2)
         nc.sync.dma_start(out=e_codes[:].bitcast(I32), in_=we_words[0].bitcast(I32))
-        nc.sync.dma_start(out=b_codes[:].bitcast(I32), in_=wb_words.rearrange("a p n -> p a n").bitcast(I32))
-        for j in range(2):
-            nc.sync.dma_start(out=table_scales[j:P:8, :].bitcast(I32),
-                              in_=tab_scales[:, j:16:2, :].rearrange("a g c -> g a c").bitcast(I32))
+        nc.sync.dma_start(out=b_codes[:].bitcast(I32), in_=wb_words.rearrange("m p n -> p m n").bitcast(I32))
+        for r in range(2):
+            nc.sync.dma_start(out=table_scales[r:P:8, :].bitcast(I32),
+                              in_=tab_scales[:, r:16:2, :].rearrange("m g c -> g m c").bitcast(I32))
         load_rows(raw_a[0], wa[0:K_PASS, :])
         load_scales(bc_scales, 0, wb_scales, range(4))
         load_scales(e_scales, 0, we_scales, range(2))
         load_rows(raw_a[1], wa[K_PASS:K, :])
-        load_scales(bc_scales, 8, wc_scales, range(4))
+        load_scales(bc_scales, WC_ROW, wc_scales, range(4))
         load_scales(e_scales, 0, we_scales, range(2, 4))
         load_words(0)
 
         nc.vector.tensor_copy(out=picked_scales[:], in_=table_scales[:].indirect(gather_list[:]))
         picked_words = picked_scales[:].bitcast(I32)
         nc.vector.tensor_copy(out=v_scales[:, 0, :].bitcast(I32), in_=picked_words)
-        for a, odd in ((0, 1), (1, 0), (1, 1)):
-            for j in range(2):
-                nc.sync.dma_start(out=v_scales[2 * odd + j : P : 32, a, :].bitcast(I32),
-                                  in_=picked_words[16 * odd + 8 * a + j : P : 32, :])
+        for m, odd in ((0, 1), (1, 0), (1, 1)):
+            for r in range(2):
+                nc.sync.dma_start(out=v_scales[2 * odd + r : P : 32, m, :].bitcast(I32),
+                                  in_=picked_words[16 * odd + 8 * m + r : P : 32, :])
 
         load_words(1)
-        nc.sync.dma_start(out=c_codes[:], in_=wc_words.rearrange("a p n t -> p a (n t)").bitcast(I32))
+        nc.sync.dma_start(out=c_codes[:], in_=wc_words.rearrange("m p n t -> p m (n t)").bitcast(I32))
         load_rows(raw_d, wd)
         load_rows(raw_f, wf)
         nc.sync.dma_start(out=weights[:], in_=wgo)
 
         v_codes = {}
 
-        def gather_words(a, g):
-            v_codes[a, g] = keep.tile([P, GATHER], U32, name=f"v_codes{a}_{g}", align_bytes=64)
-            cols = slice(g * GATHER // PER_COLUMN, (g + 1) * GATHER // PER_COLUMN)
-            nc.vector.tensor_copy(out=v_codes[a, g][:], in_=table[a][:].bitcast(U32).indirect(gather_list[:, cols]))
+        def gather_words(m, part):
+            v_codes[m, part] = keep.tile([P, GATHER], U32, name=f"v_codes{m}_{part}", align_bytes=64)
+            cols = slice(part * GATHER // PER_COLUMN, (part + 1) * GATHER // PER_COLUMN)
+            nc.vector.tensor_copy(out=v_codes[m, part][:], in_=table[m][:].bitcast(U32).indirect(gather_list[:, cols]))
 
-        def quantize_weight(raw, codes, scales, copies):
-            width = H // len(copies)
+        def quantize_weight(raw, codes, scales, shares):
+            width = raw.shape[2] // len(shares)
             rounded = []
-            for i, (copy, tag) in enumerate(copies):
+            for i, (copy, tag) in enumerate(shares):
                 tile = keep.tile([P, PACK * width], BF16, name="rounded", tag=tag, align_bytes=64)
                 copy(out=interleaved(tile[:]), in_=by_rows(raw[:, :, i * width : (i + 1) * width]))
                 rounded.append(tile)
@@ -142,20 +145,20 @@ def tile_list_seat_hand_values_kernel(tc, tab_words, tab_scales, offs, wa, wb_wo
                 cols = slice(i * width, (i + 1) * width)
                 nc.vector.quantize_mx(out=codes[:, cols].bitcast(FP8X4), scales=scales[:, cols], in_=tile[:])
 
-        for a in range(PASSES):
-            quantize_weight(raw_a[a], a_codes[a], a_scales[:, a, :], [(nc.scalar.copy, f"rounded_a{a}")])
-        for g in range(S // GATHER):
-            for a in range(PASSES):
-                gather_words(a, g)
+        for m in range(PASSES):
+            quantize_weight(raw_a[m], a_codes[m], a_scales[:, m, :], [(nc.scalar.copy, f"rounded_a{m}")])
+        for part in range(S // GATHER):
+            for m in range(PASSES):
+                gather_words(m, part)
 
-        turns = {"first": [], "second": [], "third": []}
+        banks = {"be": [], "ad": [], "cf": []}
 
         def product(kind, lhs, rhs):
-            bank = psum.tile([P, K_PASS], F32, name="bank", tag=f"{kind}{len(turns[kind]) % 2}")
-            turns[kind].append(bank)
-            for a, ((codes, scales), (w_codes, w_scales)) in enumerate(zip(lhs, rhs)):
+            bank = psum.tile([P, K_PASS], F32, name="bank", tag=f"{kind}{len(banks[kind]) % 2}")
+            banks[kind].append(bank)
+            for m, ((codes, scales), (w_codes, w_scales)) in enumerate(zip(lhs, rhs)):
                 nc.tensor.matmul_mx(out=bank[:], lhsT=codes, lhsT_scale=scales, rhs=w_codes, rhs_scale=w_scales,
-                                    start=(a == 0), stop=(a == len(lhs) - 1))
+                                    start=(m == 0), stop=(m == len(lhs) - 1))
             return bank
 
         def copied(tag, view):
@@ -176,29 +179,32 @@ def tile_list_seat_hand_values_kernel(tc, tab_words, tab_scales, offs, wa, wb_wo
                                      start=(i == 0), stop=(i == len(terms) - 1))
             return bank
 
-        h_terms, h, y_terms = {}, {}, {}
+        ab, h_terms, h, y_terms = {}, {}, {}, {}
 
         def picked(s):
-            g, first = divmod(s * P, GATHER)
-            return [(v_codes[a, g][:, first : first + P].bitcast(FP8X4), v_scales[:, a, s * P : (s + 1) * P])
-                    for a in range(PASSES)]
-
-        ab = {}
+            part, first = divmod(s * P, GATHER)
+            return [(v_codes[m, part][:, first : first + P].bitcast(FP8X4), v_scales[:, m, s * P : (s + 1) * P])
+                    for m in range(PASSES)]
 
         def feature_product(s):
-            b_bank = product("first", picked(s), [(b_codes[:, a, :].bitcast(FP4X4), bc_scales[:, a, :])
-                                                  for a in range(PASSES)])
-            b = copied(f"b{s % 3}", by_pair(b_bank))
-            a_bank = product("second", picked(s), [(a_codes[a][:].bitcast(FP8X4), a_scales[:, a, :])
-                                                   for a in range(PASSES)])
-            ab[s] = times(f"ab{s % 2}", by_pair(a_bank), b)
+            order = by_pair if s < ADDED_ON_VECTOR else by_slice
+            b_bank = product("be", picked(s), [(b_codes[:, m, :].bitcast(FP4X4), bc_scales[:, m, :])
+                                               for m in range(PASSES)])
+            b = copied(f"b{s % 3}", order(b_bank))
+            a_bank = product("ad", picked(s), [(a_codes[m][:].bitcast(FP8X4), a_scales[:, m, :])
+                                               for m in range(PASSES)])
+            ab[s] = times(f"ab{s % 2}", order(a_bank), b)
 
         def feature_sum(s):
-            c_bank = product("third", picked(s), [(c_codes[:, a, :].bitcast(FP8X4), bc_scales[8:P, a, :])
-                                                  for a in range(PASSES)])
-            pairs = keep.tile([P, 2, P, 2], BF16, name="pairs", tag=f"pairs{s % 2}", align_bytes=64)
-            nc.vector.tensor_tensor(out=pairs[:], in0=by_pair(c_bank), in1=ab[s][:], op=ADD)
-            h_terms[s] = [pairs[:].rearrange("j u p e -> j (u p e)").bitcast(F32).rearrange("j (u p) -> j u p", u=2)]
+            c_bank = product("cf", picked(s), [(c_codes[:, m, :].bitcast(FP8X4), bc_scales[WC_ROW:P, m, :])
+                                               for m in range(PASSES)])
+            if s < ADDED_ON_VECTOR:
+                pairs = keep.tile([P, 2, P, 2], BF16, name="pairs", tag=f"pairs{s % 2}", align_bytes=64)
+                nc.vector.tensor_tensor(out=pairs[:], in0=by_pair(c_bank), in1=ab[s][:], op=ADD)
+                words = pairs[:].rearrange("j u p e -> j (u p e)").bitcast(F32)
+                h_terms[s] = [words.rearrange("j (u p) -> j u p", u=2)]
+            else:
+                h_terms[s] = [copied(f"c{s % 2}", by_slice(c_bank))[:], ab[s][:]]
 
         def features(s):
             feature_product(s)
@@ -207,17 +213,21 @@ def tile_list_seat_hand_values_kernel(tc, tab_words, tab_scales, offs, wa, wb_wo
         def quantize_features(s):
             bank = turned_sum("h_bank", h_terms[s])
             rounded = ring.tile([P, P * PACK], BF16, name="h_rounded", align_bytes=64)
-            nc.scalar.copy(out=rounded[:].bitcast(F32).rearrange("p (j u) -> p j u", u=2),
-                           in_=bank[:, 0:2, :].rearrange("p u j -> p j u"))
-            codes = keep.tile([P, P], U32, name="h_codes", tag=f"h_codes{s}", align_bytes=64)
+            if s < ADDED_ON_VECTOR:
+                nc.scalar.copy(out=rounded[:].bitcast(F32).rearrange("p (j u) -> p j u", u=2),
+                               in_=bank[:, 0:2, :].rearrange("p u j -> p j u"))
+            else:
+                nc.scalar.copy(out=rounded[:].rearrange("p (j t) -> p j t", t=PACK),
+                               in_=bank[:].rearrange("p t j -> p j t"))
+            codes = keep.tile([P, P], U32, name=f"h_codes{s}", align_bytes=64)
             scales = keep.tile([P, P], U8, name=f"h_scales{s}", align_bytes=64)
             nc.vector.quantize_mx(out=codes[:].bitcast(FP8X4), scales=scales[:], in_=rounded[:])
             h[s] = [(codes[:].bitcast(FP8X4), scales[:])]
 
         def values(s):
-            e = copied(f"e{s % 2}", by_slice(product("first", h[s], [(e_codes[:].bitcast(FP4X4), e_scales[:, 0, :])])))
-            de = times(f"de{s % 3}", by_slice(product("second", h[s], [(d_codes[:].bitcast(FP8X4), d_scales[:])])), e)
-            f = copied(f"f{s % 3}", by_slice(product("third", h[s], [(f_codes[:].bitcast(FP8X4), f_scales[:])])))
+            e = copied(f"e{s % 2}", by_slice(product("be", h[s], [(e_codes[:].bitcast(FP4X4), e_scales[:, 0, :])])))
+            de = times(f"de{s % 3}", by_slice(product("ad", h[s], [(d_codes[:].bitcast(FP8X4), d_scales[:])])), e)
+            f = copied(f"f{s % 3}", by_slice(product("cf", h[s], [(f_codes[:].bitcast(FP8X4), f_scales[:])])))
             y_terms[s] = [f[:], de[:]]
 
         y = keep.tile([P, PACK, S], F32, name="y")
@@ -226,9 +236,9 @@ def tile_list_seat_hand_values_kernel(tc, tab_words, tab_scales, offs, wa, wb_wo
             bank = turned_sum("y_bank", y_terms[s])
             nc.scalar.copy(out=y[:, :, s * P : (s + 1) * P], in_=bank[:])
             for t in range(PACK):
-                held = TILES - (HELD if t == PACK - 1 else 1)
-                if s < held or s == TILES - 1:
-                    lo, hi = min(s, held) * P, (s + 1) * P
+                first_held = TILES - (HELD if t == PACK - 1 else 1)
+                if s < first_held or s == TILES - 1:
+                    lo, hi = min(s, first_held) * P, (s + 1) * P
                     window = pages[t][:].indirect(scatter_list[:, lo // PER_COLUMN : hi // PER_COLUMN])
                     nc.vector.tensor_tensor(out=window, in0=y[:, t, lo:hi], in1=weights[:, lo:hi], op=MULT)
                 if s == TILES - 1:
@@ -241,8 +251,8 @@ def tile_list_seat_hand_values_kernel(tc, tab_words, tab_scales, offs, wa, wb_wo
         for stage, s in ((values, 0), (place_values, 0), (features, 2), (quantize_features, 1), (values, 1),
                          (features, 3), (quantize_features, 2)):
             stage(s)
-        for j in range(1, TILES):
-            for stage, s in ((feature_product, j + 3), (values, j + 1), (feature_sum, j + 3),
-                             (quantize_features, j + 2), (place_values, j)):
+        for step in range(1, TILES):
+            for stage, s in ((feature_product, step + LEAD), (values, step + 1), (feature_sum, step + LEAD),
+                             (quantize_features, step + LEAD - 1), (place_values, step)):
                 if s < TILES:
                     stage(s)

@@ -27,7 +27,8 @@ PER_COLUMN = 16
 WC_ROW = 8
 LEAD = 3
 HELD = 6
-ADDED_ON_VECTOR = 5
+ADDED_ON_VECTOR = 8
+ON_VECTOR = 1
 
 
 def interleaved(tile):
@@ -226,7 +227,13 @@ def tile_list_seat_hand_values_kernel(tc, tab_words, tab_scales, offs, wa, wb_wo
 
         def values(s):
             e = copied(f"e{s % 2}", by_slice(product("be", h[s], [(e_codes[:].bitcast(FP4X4), e_scales[:, 0, :])])))
-            de = times(f"de{s % 3}", by_slice(product("ad", h[s], [(d_codes[:].bitcast(FP8X4), d_scales[:])])), e)
+            d = by_slice(product("ad", h[s], [(d_codes[:].bitcast(FP8X4), d_scales[:])]))
+            if s < ON_VECTOR:
+                de = times(f"de{s % 3}", d, e)
+            else:
+                d = copied(f"d{s % 2}", d)
+                de = keep.tile([P, PACK, P], F32, name="times", tag=f"de{s % 3}", align_bytes=64)
+                nc.gpsimd.tensor_tensor(out=de[:], in0=d[:], in1=e[:], op=MULT)
             f = copied(f"f{s % 3}", by_slice(product("cf", h[s], [(f_codes[:].bitcast(FP8X4), f_scales[:])])))
             y_terms[s] = [f[:], de[:]]
 
@@ -234,13 +241,18 @@ def tile_list_seat_hand_values_kernel(tc, tab_words, tab_scales, offs, wa, wb_wo
 
         def place_values(s):
             bank = turned_sum("y_bank", y_terms[s])
-            nc.scalar.copy(out=y[:, :, s * P : (s + 1) * P], in_=bank[:])
+            lines = slice(s * P, (s + 1) * P)
+            weight = weights[:, lines].unsqueeze(1).to_broadcast([P, PACK, P])
+            if s < ON_VECTOR:
+                nc.vector.tensor_tensor(out=y[:, :, lines], in0=bank[:], in1=weight, op=MULT)
+            else:
+                nc.gpsimd.tensor_tensor(out=y[:, :, lines], in0=copied(f"y{s % 2}", bank[:])[:], in1=weight, op=MULT)
             for t in range(PACK):
                 first_held = TILES - (HELD if t == PACK - 1 else 1)
                 if s < first_held or s == TILES - 1:
                     lo, hi = min(s, first_held) * P, (s + 1) * P
                     window = pages[t][:].indirect(scatter_list[:, lo // PER_COLUMN : hi // PER_COLUMN])
-                    nc.vector.tensor_tensor(out=window, in0=y[:, t, lo:hi], in1=weights[:, lo:hi], op=MULT)
+                    nc.vector.tensor_copy(out=window, in_=y[:, t, lo:hi])
                 if s == TILES - 1:
                     nc.sync.dma_start(out=out.rearrange("(p t) c -> p t c", t=PACK)[:, t, :], in_=pages[t][:])
 

@@ -27,7 +27,7 @@ PER_COLUMN = 16
 WC_ROW = 8
 LEAD = 3
 HELD = 6
-ADDED_ON_VECTOR = 8
+ADDED_ON_VECTOR = 3
 ON_VECTOR = 1
 
 
@@ -71,6 +71,7 @@ def tile_list_seat_hand_values_kernel(tc, tab_words, tab_scales, offs, wa, wb_wo
         c_codes = keep.tile([P, PASSES, H], I32, name="c_codes", align_bytes=64)
         e_codes = keep.tile([P, 2 * N], U8, name="e_codes", align_bytes=64)
         bc_scales = keep.tile([P, PASSES, H], U8, name="bc_scales", align_bytes=64)
+        c_scales = keep.tile([P, PASSES, H], U8, name="c_scales", align_bytes=64)
         a_scales = keep.tile([P, PASSES, H], U8, name="a_scales", align_bytes=64)
         d_scales = keep.tile([P, N], U8, name="d_scales", align_bytes=64)
         e_scales = keep.tile([P, 1, N], U8, name="e_scales", align_bytes=64)
@@ -90,29 +91,25 @@ def tile_list_seat_hand_values_kernel(tc, tab_words, tab_scales, offs, wa, wb_wo
                 nc.sync.dma_start(out=tile[first + r : P : 32].bitcast(I32),
                                   in_=scales[:, r:16:4, :].rearrange("m q c -> q m c").bitcast(I32))
 
-        nc.gpsimd.memset(table_scales[:].bitcast(I32), 0)
-        nc.gpsimd.memset(bc_scales[:].rearrange("p m c -> p (m c)").bitcast(I32), 0)
-        nc.gpsimd.memset(e_scales[:].rearrange("p m c -> p (m c)").bitcast(I32), 0)
-        nc.gpsimd.memset(v_scales[:, 1, :].bitcast(I32), 0)
+        nc.vector.memset(table_scales[:].bitcast(I32), 0)
+        nc.vector.memset(bc_scales[:].rearrange("p m c -> p (m c)").bitcast(I32), 0)
+        nc.vector.memset(c_scales[:].rearrange("p m c -> p (m c)").bitcast(I32), 0)
+        nc.vector.memset(e_scales[:].rearrange("p m c -> p (m c)").bitcast(I32), 0)
+        nc.vector.memset(v_scales[:, 1, :].bitcast(I32), 0)
         make_identity(nc, identity[:])
-        for page in pages:
-            for half in range(2):
-                nc.gpsimd.memset(page[:, half * T2 // 2 : (half + 1) * T2 // 2].bitcast(I32), 0)
+        for t, page in enumerate(pages):
+            for i in range(4):
+                engine = nc.vector if t < 0 else nc.gpsimd
+                engine.memset(page[:, i * T2 // 4 : (i + 1) * T2 // 4].bitcast(I32), 0)
 
         nc.sync.dma_start(out=gather_list[:], in_=offs)
-        nc.sync.dma_start(out=scatter_list[:], in_=offs2)
-        nc.sync.dma_start(out=e_codes[:].bitcast(I32), in_=we_words[0].bitcast(I32))
         nc.sync.dma_start(out=b_codes[:].bitcast(I32), in_=wb_words.rearrange("m p n -> p m n").bitcast(I32))
         for r in range(2):
             nc.sync.dma_start(out=table_scales[r:P:8, :].bitcast(I32),
                               in_=tab_scales[:, r:16:2, :].rearrange("m g c -> g m c").bitcast(I32))
-        load_rows(raw_a[0], wa[0:K_PASS, :])
-        load_scales(bc_scales, 0, wb_scales, range(4))
-        load_scales(e_scales, 0, we_scales, range(2))
-        load_rows(raw_a[1], wa[K_PASS:K, :])
-        load_scales(bc_scales, WC_ROW, wc_scales, range(4))
-        load_scales(e_scales, 0, we_scales, range(2, 4))
         load_words(0)
+        load_scales(bc_scales, 0, wb_scales, range(4))
+        load_words(1)
 
         nc.vector.tensor_copy(out=picked_scales[:], in_=table_scales[:].indirect(gather_list[:]))
         picked_words = picked_scales[:].bitcast(I32)
@@ -122,10 +119,16 @@ def tile_list_seat_hand_values_kernel(tc, tab_words, tab_scales, offs, wa, wb_wo
                 nc.sync.dma_start(out=v_scales[2 * odd + r : P : 32, m, :].bitcast(I32),
                                   in_=picked_words[16 * odd + 8 * m + r : P : 32, :])
 
-        load_words(1)
-        nc.sync.dma_start(out=c_codes[:], in_=wc_words.rearrange("m p n t -> p m (n t)").bitcast(I32))
+        load_rows(raw_a[0], wa[0:K_PASS, :])
+        load_scales(c_scales, 0, wc_scales, range(4))
+        load_scales(e_scales, 0, we_scales, range(2))
+        load_rows(raw_a[1], wa[K_PASS:K, :])
         load_rows(raw_d, wd)
+        nc.sync.dma_start(out=c_codes[:], in_=wc_words.rearrange("m p n t -> p m (n t)").bitcast(I32))
         load_rows(raw_f, wf)
+        load_scales(e_scales, 0, we_scales, range(2, 4))
+        nc.sync.dma_start(out=e_codes[:].bitcast(I32), in_=we_words[0].bitcast(I32))
+        nc.sync.dma_start(out=scatter_list[:], in_=offs2)
         nc.sync.dma_start(out=weights[:], in_=wgo)
 
         v_codes = {}
@@ -146,17 +149,15 @@ def tile_list_seat_hand_values_kernel(tc, tab_words, tab_scales, offs, wa, wb_wo
                 cols = slice(i * width, (i + 1) * width)
                 nc.vector.quantize_mx(out=codes[:, cols].bitcast(FP8X4), scales=scales[:, cols], in_=tile[:])
 
-        for m in range(PASSES):
-            quantize_weight(raw_a[m], a_codes[m], a_scales[:, m, :], [(nc.scalar.copy, f"rounded_a{m}")])
         for part in range(S // GATHER):
             for m in range(PASSES):
                 gather_words(m, part)
+        for m in range(PASSES):
+            quantize_weight(raw_a[m], a_codes[m], a_scales[:, m, :],
+                            [(nc.vector.tensor_copy, f"rounded_a{m}{i}") for i in range(2)])
 
-        banks = {"be": [], "ad": [], "cf": []}
-
-        def product(kind, lhs, rhs):
-            bank = psum.tile([P, K_PASS], F32, name="bank", tag=f"{kind}{len(banks[kind]) % 2}")
-            banks[kind].append(bank)
+        def product(tag, lhs, rhs):
+            bank = psum.tile([P, K_PASS], F32, name="bank", tag=tag)
             for m, ((codes, scales), (w_codes, w_scales)) in enumerate(zip(lhs, rhs)):
                 nc.tensor.matmul_mx(out=bank[:], lhsT=codes, lhsT_scale=scales, rhs=w_codes, rhs_scale=w_scales,
                                     start=(m == 0), stop=(m == len(lhs) - 1))
@@ -180,24 +181,28 @@ def tile_list_seat_hand_values_kernel(tc, tab_words, tab_scales, offs, wa, wb_wo
                                      start=(i == 0), stop=(i == len(terms) - 1))
             return bank
 
-        ab, h_terms, h, y_terms = {}, {}, {}, {}
+        b, ab, h_terms, h, y_terms = {}, {}, {}, {}, {}
 
         def picked(s):
             part, first = divmod(s * P, GATHER)
             return [(v_codes[m, part][:, first : first + P].bitcast(FP8X4), v_scales[:, m, s * P : (s + 1) * P])
                     for m in range(PASSES)]
 
+        def order(s):
+            return by_pair if s < ADDED_ON_VECTOR else by_slice
+
+        def feature_factor(s):
+            b_bank = product("cedf"[s % 4], picked(s), [(b_codes[:, m, :].bitcast(FP4X4), bc_scales[:, m, :])
+                                               for m in range(PASSES)])
+            b[s] = copied(f"b{s}", order(s)(b_bank))
+
         def feature_product(s):
-            order = by_pair if s < ADDED_ON_VECTOR else by_slice
-            b_bank = product("be", picked(s), [(b_codes[:, m, :].bitcast(FP4X4), bc_scales[:, m, :])
-                                               for m in range(PASSES)])
-            b = copied(f"b{s % 3}", order(b_bank))
-            a_bank = product("ad", picked(s), [(a_codes[m][:].bitcast(FP8X4), a_scales[:, m, :])
-                                               for m in range(PASSES)])
-            ab[s] = times(f"ab{s % 2}", order(a_bank), b)
+            a_bank = product(f"a{s % 2}", picked(s), [(a_codes[m][:].bitcast(FP8X4), a_scales[:, m, :])
+                                              for m in range(PASSES)])
+            ab[s] = times(f"ab{s % 2}", order(s)(a_bank), b[s])
 
         def feature_sum(s):
-            c_bank = product("cf", picked(s), [(c_codes[:, m, :].bitcast(FP8X4), bc_scales[WC_ROW:P, m, :])
+            c_bank = product("y_bank" if s == 1 else "c", picked(s), [(c_codes[:, m, :].bitcast(FP8X4), c_scales[:, m, :])
                                                for m in range(PASSES)])
             if s < ADDED_ON_VECTOR:
                 pairs = keep.tile([P, 2, P, 2], BF16, name="pairs", tag=f"pairs{s % 2}", align_bytes=64)
@@ -226,15 +231,15 @@ def tile_list_seat_hand_values_kernel(tc, tab_words, tab_scales, offs, wa, wb_wo
             h[s] = [(codes[:].bitcast(FP8X4), scales[:])]
 
         def values(s):
-            e = copied(f"e{s % 2}", by_slice(product("be", h[s], [(e_codes[:].bitcast(FP4X4), e_scales[:, 0, :])])))
-            d = by_slice(product("ad", h[s], [(d_codes[:].bitcast(FP8X4), d_scales[:])]))
-            if s < ON_VECTOR:
+            e = copied(f"e{s % 2}", by_slice(product("e", h[s], [(e_codes[:].bitcast(FP4X4), e_scales[:, 0, :])])))
+            d = by_slice(product("d", h[s], [(d_codes[:].bitcast(FP8X4), d_scales[:])]))
+            if s < ON_VECTOR + 1:
                 de = times(f"de{s % 3}", d, e)
             else:
                 d = copied(f"d{s % 2}", d)
                 de = keep.tile([P, PACK, P], F32, name="times", tag=f"de{s % 3}", align_bytes=64)
                 nc.gpsimd.tensor_tensor(out=de[:], in0=d[:], in1=e[:], op=MULT)
-            f = copied(f"f{s % 3}", by_slice(product("cf", h[s], [(f_codes[:].bitcast(FP8X4), f_scales[:])])))
+            f = copied(f"f{s % 3}", by_slice(product("f", h[s], [(f_codes[:].bitcast(FP8X4), f_scales[:])])))
             y_terms[s] = [f[:], de[:]]
 
         y = keep.tile([P, PACK, S], F32, name="y")
@@ -256,15 +261,15 @@ def tile_list_seat_hand_values_kernel(tc, tab_words, tab_scales, offs, wa, wb_wo
                 if s == TILES - 1:
                     nc.sync.dma_start(out=out.rearrange("(p t) c -> p t c", t=PACK)[:, t, :], in_=pages[t][:])
 
-        for stage, s in ((features, 0), (features, 1), (quantize_features, 0)):
+        for s in range(TILES):
+            feature_factor(s)
+        for stage, s in ((features, 0), (features, 1), (quantize_features, 0), (quantize_features, 1)):
             stage(s)
         quantize_weight(raw_d, d_codes, d_scales[:], [(nc.scalar.copy, "rounded_d0"), (nc.scalar.copy, "rounded_d1")])
-        quantize_weight(raw_f, f_codes, f_scales[:], [(nc.vector.tensor_copy, "ab1"), (nc.scalar.copy, "rounded_f1")])
-        for stage, s in ((values, 0), (place_values, 0), (features, 2), (quantize_features, 1), (values, 1),
-                         (features, 3), (quantize_features, 2)):
+        quantize_weight(raw_f, f_codes, f_scales[:], [(nc.vector.tensor_copy, "rounded_f0"), (nc.scalar.copy, "rounded_f1")])
+        for stage, s in ((values, 0), (features, 2), (values, 1), (quantize_features, 2), (place_values, 0), (features, 3), (quantize_features, 3), (features, 4),):
             stage(s)
         for step in range(1, TILES):
-            for stage, s in ((feature_product, step + LEAD), (values, step + 1), (feature_sum, step + LEAD),
-                             (quantize_features, step + LEAD - 1), (place_values, step)):
+            for stage, s in ((feature_product, step + 4), (values, step + 1), (feature_sum, step + 4), (place_values, step + 0), (quantize_features, step + 3)):
                 if s < TILES:
                     stage(s)

@@ -27,7 +27,7 @@ PER_COLUMN = 16
 WC_ROW = 8
 LEAD = 3
 HELD = 6
-ADDED_ON_VECTOR = 3
+ADDED_ON_VECTOR = 4
 ON_VECTOR = 1
 
 
@@ -103,12 +103,13 @@ def tile_list_seat_hand_values_kernel(tc, tab_words, tab_scales, offs, wa, wb_wo
                 engine.memset(page[:, i * T2 // 4 : (i + 1) * T2 // 4].bitcast(I32), 0)
 
         nc.sync.dma_start(out=gather_list[:], in_=offs)
-        nc.sync.dma_start(out=b_codes[:].bitcast(I32), in_=wb_words.rearrange("m p n -> p m n").bitcast(I32))
+        nc.sync.dma_start(out=scatter_list[:], in_=offs2)
         for r in range(2):
             nc.sync.dma_start(out=table_scales[r:P:8, :].bitcast(I32),
                               in_=tab_scales[:, r:16:2, :].rearrange("m g c -> g m c").bitcast(I32))
         load_words(0)
         load_scales(bc_scales, 0, wb_scales, range(4))
+        nc.sync.dma_start(out=b_codes[:].bitcast(I32), in_=wb_words.rearrange("m p n -> p m n").bitcast(I32))
         load_words(1)
 
         nc.vector.tensor_copy(out=picked_scales[:], in_=table_scales[:].indirect(gather_list[:]))
@@ -123,12 +124,11 @@ def tile_list_seat_hand_values_kernel(tc, tab_words, tab_scales, offs, wa, wb_wo
         load_scales(c_scales, 0, wc_scales, range(4))
         load_scales(e_scales, 0, we_scales, range(2))
         load_rows(raw_a[1], wa[K_PASS:K, :])
-        load_rows(raw_d, wd)
         nc.sync.dma_start(out=c_codes[:], in_=wc_words.rearrange("m p n t -> p m (n t)").bitcast(I32))
+        load_rows(raw_d, wd)
         load_rows(raw_f, wf)
         load_scales(e_scales, 0, we_scales, range(2, 4))
         nc.sync.dma_start(out=e_codes[:].bitcast(I32), in_=we_words[0].bitcast(I32))
-        nc.sync.dma_start(out=scatter_list[:], in_=offs2)
         nc.sync.dma_start(out=weights[:], in_=wgo)
 
         v_codes = {}
@@ -232,13 +232,7 @@ def tile_list_seat_hand_values_kernel(tc, tab_words, tab_scales, offs, wa, wb_wo
 
         def values(s):
             e = copied(f"e{s % 2}", by_slice(product("e", h[s], [(e_codes[:].bitcast(FP4X4), e_scales[:, 0, :])])))
-            d = by_slice(product("d", h[s], [(d_codes[:].bitcast(FP8X4), d_scales[:])]))
-            if s < ON_VECTOR + 1:
-                de = times(f"de{s % 3}", d, e)
-            else:
-                d = copied(f"d{s % 2}", d)
-                de = keep.tile([P, PACK, P], F32, name="times", tag=f"de{s % 3}", align_bytes=64)
-                nc.gpsimd.tensor_tensor(out=de[:], in0=d[:], in1=e[:], op=MULT)
+            de = times(f"de{s % 3}", by_slice(product("d", h[s], [(d_codes[:].bitcast(FP8X4), d_scales[:])])), e)
             f = copied(f"f{s % 3}", by_slice(product("f", h[s], [(f_codes[:].bitcast(FP8X4), f_scales[:])])))
             y_terms[s] = [f[:], de[:]]
 
@@ -246,18 +240,13 @@ def tile_list_seat_hand_values_kernel(tc, tab_words, tab_scales, offs, wa, wb_wo
 
         def place_values(s):
             bank = turned_sum("y_bank", y_terms[s])
-            lines = slice(s * P, (s + 1) * P)
-            weight = weights[:, lines].unsqueeze(1).to_broadcast([P, PACK, P])
-            if s < ON_VECTOR:
-                nc.vector.tensor_tensor(out=y[:, :, lines], in0=bank[:], in1=weight, op=MULT)
-            else:
-                nc.gpsimd.tensor_tensor(out=y[:, :, lines], in0=copied(f"y{s % 2}", bank[:])[:], in1=weight, op=MULT)
+            nc.scalar.copy(out=y[:, :, s * P : (s + 1) * P], in_=bank[:])
             for t in range(PACK):
                 first_held = TILES - (HELD if t == PACK - 1 else 1)
                 if s < first_held or s == TILES - 1:
                     lo, hi = min(s, first_held) * P, (s + 1) * P
                     window = pages[t][:].indirect(scatter_list[:, lo // PER_COLUMN : hi // PER_COLUMN])
-                    nc.vector.tensor_copy(out=window, in_=y[:, t, lo:hi])
+                    nc.vector.tensor_tensor(out=window, in0=y[:, t, lo:hi], in1=weights[:, lo:hi], op=MULT)
                 if s == TILES - 1:
                     nc.sync.dma_start(out=out.rearrange("(p t) c -> p t c", t=PACK)[:, t, :], in_=pages[t][:])
 

@@ -26,7 +26,7 @@ GATHER = 256
 PER_COLUMN = 16
 WC_ROW = 8
 LEAD = 3
-HELD = 6
+HELD = (1, 1, 1, 8)
 ADDED_ON_VECTOR = 4
 ON_VECTOR = 1
 
@@ -242,7 +242,7 @@ def tile_list_seat_hand_values_kernel(tc, tab_words, tab_scales, offs, wa, wb_wo
             bank = turned_sum("y_bank", y_terms[s])
             nc.scalar.copy(out=y[:, :, s * P : (s + 1) * P], in_=bank[:])
             for t in range(PACK):
-                first_held = TILES - (HELD if t == PACK - 1 else 1)
+                first_held = TILES - HELD[t]
                 if s < first_held or s == TILES - 1:
                     lo, hi = min(s, first_held) * P, (s + 1) * P
                     window = pages[t][:].indirect(scatter_list[:, lo // PER_COLUMN : hi // PER_COLUMN])

@@ -57,7 +57,7 @@ def tile_list_seat_hand_values_kernel(tc, tab_words, tab_scales, offs, wa, wb_wo
 
         gather_list = keep.tile([P, S // PER_COLUMN], U16, name="gather_list")
         scatter_list = keep.tile([P, S // PER_COLUMN], U16, name="scatter_list")
-        table = [keep.tile([P, T], I32, name=f"table{m}") for m in range(PASSES)]
+        table = [keep.tile([P, T], I32, name=f"table{m}", align_bytes=64) for m in range(PASSES)]
         table_scales = keep.tile([P, T], U8, name="table_scales")
         picked_scales = keep.tile([P, S], U8, name="picked_scales")
         v_scales = keep.tile([P, PASSES, S], U8, name="v_scales", align_bytes=64)
@@ -77,8 +77,13 @@ def tile_list_seat_hand_values_kernel(tc, tab_words, tab_scales, offs, wa, wb_wo
         e_scales = keep.tile([P, 1, N], U8, name="e_scales", align_bytes=64)
         f_scales = keep.tile([P, N], U8, name="f_scales", align_bytes=64)
         weights = keep.tile([P, S], F32, name="weights")
-        pages = [keep.tile([P, T2], F32, name=f"page{t}") for t in range(PACK)]
+        pages = {}
         identity = keep.tile([P, P], F32, name="identity")
+
+        def clear_page(engine, t, tag, pieces=1):
+            pages[t] = keep.tile([P, T2], F32, name="page", tag=tag, align_bytes=64)
+            for i in range(pieces):
+                engine.memset(pages[t][:, i * T2 // pieces : (i + 1) * T2 // pieces].bitcast(I32), 0)
 
         def load_words(m):
             nc.sync.dma_start(out=table[m][:], in_=tab_words[m].rearrange("p n t -> p (n t)").bitcast(I32))
@@ -86,10 +91,10 @@ def tile_list_seat_hand_values_kernel(tc, tab_words, tab_scales, offs, wa, wb_wo
         def load_rows(raw, rows):
             nc.sync.dma_start(out=raw[:], in_=rows.rearrange("(p t) c -> p t c", t=PACK))
 
-        def load_scales(tile, first, scales, rows):
+        def load_scales(queue, tile, first, scales, rows):
             for r in rows:
-                nc.sync.dma_start(out=tile[first + r : P : 32].bitcast(I32),
-                                  in_=scales[:, r:16:4, :].rearrange("m q c -> q m c").bitcast(I32))
+                queue.dma_start(out=tile[first + r : P : 32].bitcast(I32),
+                                in_=scales[:, r:16:4, :].rearrange("m q c -> q m c").bitcast(I32))
 
         nc.vector.memset(table_scales[:].bitcast(I32), 0)
         nc.vector.memset(bc_scales[:].rearrange("p m c -> p (m c)").bitcast(I32), 0)
@@ -97,10 +102,8 @@ def tile_list_seat_hand_values_kernel(tc, tab_words, tab_scales, offs, wa, wb_wo
         nc.vector.memset(e_scales[:].rearrange("p m c -> p (m c)").bitcast(I32), 0)
         nc.vector.memset(v_scales[:, 1, :].bitcast(I32), 0)
         make_identity(nc, identity[:])
-        for t, page in enumerate(pages):
-            for i in range(4):
-                engine = nc.vector if t < 0 else nc.gpsimd
-                engine.memset(page[:, i * T2 // 4 : (i + 1) * T2 // 4].bitcast(I32), 0)
+        for t in range(2):
+            clear_page(nc.vector, t, f"page{t}")
 
         nc.sync.dma_start(out=gather_list[:], in_=offs)
         nc.sync.dma_start(out=scatter_list[:], in_=offs2)
@@ -108,7 +111,7 @@ def tile_list_seat_hand_values_kernel(tc, tab_words, tab_scales, offs, wa, wb_wo
             nc.sync.dma_start(out=table_scales[r:P:8, :].bitcast(I32),
                               in_=tab_scales[:, r:16:2, :].rearrange("m g c -> g m c").bitcast(I32))
         load_words(0)
-        load_scales(bc_scales, 0, wb_scales, range(4))
+        load_scales(nc.sync, bc_scales, 0, wb_scales, range(4))
         nc.sync.dma_start(out=b_codes[:].bitcast(I32), in_=wb_words.rearrange("m p n -> p m n").bitcast(I32))
         load_words(1)
 
@@ -121,13 +124,12 @@ def tile_list_seat_hand_values_kernel(tc, tab_words, tab_scales, offs, wa, wb_wo
                                   in_=picked_words[16 * odd + 8 * m + r : P : 32, :])
 
         load_rows(raw_a[0], wa[0:K_PASS, :])
-        load_scales(c_scales, 0, wc_scales, range(4))
-        load_scales(e_scales, 0, we_scales, range(2))
+        load_scales(nc.gpsimd, c_scales, 0, wc_scales, range(4))
+        load_scales(nc.gpsimd, e_scales, 0, we_scales, range(4))
         load_rows(raw_a[1], wa[K_PASS:K, :])
         nc.sync.dma_start(out=c_codes[:], in_=wc_words.rearrange("m p n t -> p m (n t)").bitcast(I32))
         load_rows(raw_d, wd)
         load_rows(raw_f, wf)
-        load_scales(e_scales, 0, we_scales, range(2, 4))
         nc.sync.dma_start(out=e_codes[:].bitcast(I32), in_=we_words[0].bitcast(I32))
         nc.sync.dma_start(out=weights[:], in_=wgo)
 
@@ -155,6 +157,8 @@ def tile_list_seat_hand_values_kernel(tc, tab_words, tab_scales, offs, wa, wb_wo
         for m in range(PASSES):
             quantize_weight(raw_a[m], a_codes[m], a_scales[:, m, :],
                             [(nc.vector.tensor_copy, f"rounded_a{m}{i}") for i in range(2)])
+
+        clear_page(nc.gpsimd, 2, "rounded_a11", 4)
 
         def product(tag, lhs, rhs):
             bank = psum.tile([P, K_PASS], F32, name="bank", tag=tag)
@@ -200,6 +204,8 @@ def tile_list_seat_hand_values_kernel(tc, tab_words, tab_scales, offs, wa, wb_wo
             a_bank = product(f"a{s % 2}", picked(s), [(a_codes[m][:].bitcast(FP8X4), a_scales[:, m, :])
                                               for m in range(PASSES)])
             ab[s] = times(f"ab{s % 2}", order(s)(a_bank), b[s])
+            if s == TILES - 1:
+                clear_page(nc.gpsimd, PACK - 1, f"b{s}", 4)
 
         def feature_sum(s):
             c_bank = product("y_bank" if s == 1 else "c", picked(s), [(c_codes[:, m, :].bitcast(FP8X4), c_scales[:, m, :])

@@ -124,12 +124,13 @@ def tile_list_seat_hand_values_kernel(tc, tab_words, tab_scales, offs, wa, wb_wo
                                   in_=picked_words[16 * odd + 8 * m + r : P : 32, :])
 
         load_rows(raw_a[0], wa[0:K_PASS, :])
-        load_scales(nc.gpsimd, c_scales, 0, wc_scales, range(4))
-        load_scales(nc.gpsimd, e_scales, 0, we_scales, range(4))
+        load_scales(nc.sync, c_scales, 0, wc_scales, range(4))
+        load_scales(nc.sync, e_scales, 0, we_scales, range(2))
         load_rows(raw_a[1], wa[K_PASS:K, :])
         nc.sync.dma_start(out=c_codes[:], in_=wc_words.rearrange("m p n t -> p m (n t)").bitcast(I32))
         load_rows(raw_d, wd)
         load_rows(raw_f, wf)
+        load_scales(nc.sync, e_scales, 0, we_scales, range(2, 4))
         nc.sync.dma_start(out=e_codes[:].bitcast(I32), in_=we_words[0].bitcast(I32))
         nc.sync.dma_start(out=weights[:], in_=wgo)
 

@@ -240,8 +240,11 @@ def tile_list_seat_hand_values_kernel(tc, tab_words, tab_scales, offs, wa, wb_wo
         def values(s):
             e = copied(f"e{s % 2}", by_slice(product("e", h[s], [(e_codes[:].bitcast(FP4X4), e_scales[:, 0, :])])))
             de = times(f"de{s % 3}", by_slice(product("d", h[s], [(d_codes[:].bitcast(FP8X4), d_scales[:])])), e)
+            y_terms[s] = [de[:]]
+
+        def value_term(s):
             f = copied(f"f{s % 3}", by_slice(product("f", h[s], [(f_codes[:].bitcast(FP8X4), f_scales[:])])))
-            y_terms[s] = [f[:], de[:]]
+            y_terms[s] = [f[:]] + y_terms[s]
 
         y = keep.tile([P, PACK, S], F32, name="y")
 
@@ -263,9 +266,9 @@ def tile_list_seat_hand_values_kernel(tc, tab_words, tab_scales, offs, wa, wb_wo
             stage(s)
         quantize_weight(raw_d, d_codes, d_scales[:], [(nc.scalar.copy, "rounded_d0"), (nc.scalar.copy, "rounded_d1")])
         quantize_weight(raw_f, f_codes, f_scales[:], [(nc.vector.tensor_copy, "rounded_f0"), (nc.scalar.copy, "rounded_f1")])
-        for stage, s in ((values, 0), (features, 2), (values, 1), (quantize_features, 2), (place_values, 0), (features, 3), (quantize_features, 3), (features, 4),):
+        for stage, s in ((values, 0), (value_term, 0), (features, 2), (values, 1), (value_term, 1), (quantize_features, 2), (place_values, 0), (features, 3), (quantize_features, 3), (features, 4),):
             stage(s)
         for step in range(1, TILES):
-            for stage, s in ((feature_product, step + 4), (values, step + 1), (feature_sum, step + 4), (place_values, step + 0), (quantize_features, step + 3)):
+            for stage, s in ((feature_product, step + 4), (values, step + 1), (place_values, step), (value_term, step + 1), (feature_sum, step + 4), (quantize_features, step + 3)):
                 if s < TILES:
                     stage(s)

@@ -26,8 +26,8 @@ GATHER = 256
 PER_COLUMN = 16
 WC_ROW = 8
 LEAD = 3
-HELD = (1, 1, 1, 8)
-ADDED_ON_VECTOR = 4
+HELD = (1, 1, 1, 7)
+ADDED_ON_VECTOR = 5
 ON_VECTOR = 1
 
 
@@ -248,17 +248,21 @@ def tile_list_seat_hand_values_kernel(tc, tab_words, tab_scales, offs, wa, wb_wo
 
         y = keep.tile([P, PACK, S], F32, name="y")
 
+        def scatter(t, lo, hi):
+            window = pages[t][:].indirect(scatter_list[:, lo // PER_COLUMN : hi // PER_COLUMN])
+            nc.vector.tensor_tensor(out=window, in0=y[:, t, lo:hi], in1=weights[:, lo:hi], op=MULT)
+            if hi == S:
+                nc.sync.dma_start(out=out.rearrange("(p t) c -> p t c", t=PACK)[:, t, :], in_=pages[t][:])
+
         def place_values(s):
             bank = turned_sum("y_bank", y_terms[s])
             nc.scalar.copy(out=y[:, :, s * P : (s + 1) * P], in_=bank[:])
-            for t in range(PACK):
-                first_held = TILES - HELD[t]
-                if s < first_held or s == TILES - 1:
-                    lo, hi = min(s, first_held) * P, (s + 1) * P
-                    window = pages[t][:].indirect(scatter_list[:, lo // PER_COLUMN : hi // PER_COLUMN])
-                    nc.vector.tensor_tensor(out=window, in0=y[:, t, lo:hi], in1=weights[:, lo:hi], op=MULT)
-                if s == TILES - 1:
-                    nc.sync.dma_start(out=out.rearrange("(p t) c -> p t c", t=PACK)[:, t, :], in_=pages[t][:])
+            for t in range(PACK - 1):
+                scatter(t, s * P, (s + 1) * P)
+            if s == 3:
+                scatter(PACK - 1, 0, 1 * P)
+            if s == TILES - 1:
+                scatter(PACK - 1, 1 * P, S)
 
         for s in range(TILES):
             feature_factor(s)

@@ -179,7 +179,7 @@ def tile_list_seat_hand_values_kernel(tc, tab_words, tab_scales, offs, wa, wb_wo
             return tile
 
         def turned_sum(name, terms):
-            bank = psum.tile([P, PACK, P], F32, name=name)
+            bank = psum.tile([P, PACK, P], F32, name="bank", tag=name)
             for t in range(terms[0].shape[1]):
                 for i, term in enumerate(terms):
                     nc.tensor.matmul(out=bank[:, t, :], lhsT=term[:, t, :], rhs=identity[:], is_transpose=True,
@@ -255,8 +255,12 @@ def tile_list_seat_hand_values_kernel(tc, tab_words, tab_scales, offs, wa, wb_wo
                 nc.sync.dma_start(out=out.rearrange("(p t) c -> p t c", t=PACK)[:, t, :], in_=pages[t][:])
 
         def place_values(s):
-            bank = turned_sum("y_bank", y_terms[s])
-            nc.scalar.copy(out=y[:, :, s * P : (s + 1) * P], in_=bank[:])
+            first = 1 if s == 0 or s >= 4 else 0
+            if first:
+                bank = turned_sum("a0" if s else "e", [term[:, :first] for term in y_terms[s]])
+                nc.scalar.copy(out=y[:, :first, s * P : (s + 1) * P], in_=bank[:, :first])
+            bank = turned_sum("y_bank", [term[:, first:] for term in y_terms[s]])
+            nc.scalar.copy(out=y[:, first:, s * P : (s + 1) * P], in_=bank[:, : PACK - first])
             for t in range(PACK - 1):
                 scatter(t, s * P, (s + 1) * P)
             if s == 3:

@@ -180,10 +180,11 @@ def tile_list_seat_hand_values_kernel(tc, tab_words, tab_scales, offs, wa, wb_wo
 
         def turned_sum(name, terms):
             bank = psum.tile([P, PACK, P], F32, name="bank", tag=name)
-            for t in range(terms[0].shape[1]):
-                for i, term in enumerate(terms):
+            slices = terms[0].shape[1]
+            for i, term in enumerate(terms):
+                for t in range(slices):
                     nc.tensor.matmul(out=bank[:, t, :], lhsT=term[:, t, :], rhs=identity[:], is_transpose=True,
-                                     start=(i == 0), stop=(i == len(terms) - 1))
+                                     start=(i == 0 and t == 0), stop=(i == len(terms) - 1 and t == slices - 1))
             return bank
 
         b, ab, h_terms, h, y_terms = {}, {}, {}, {}, {}

@@ -96,7 +96,7 @@ def tile_list_seat_hand_values_kernel(tc, tab_words, tab_scales, offs, wa, wb_wo
                 queue.dma_start(out=tile[first + r : P : 32].bitcast(I32),
                                 in_=scales[:, r:16:4, :].rearrange("m q c -> q m c").bitcast(I32))
 
-        nc.vector.memset(table_scales[:].bitcast(I32), 0)
+        nc.gpsimd.memset(table_scales[:].bitcast(I32), 0)
         nc.vector.memset(bc_scales[:].rearrange("p m c -> p (m c)").bitcast(I32), 0)
         nc.vector.memset(c_scales[:].rearrange("p m c -> p (m c)").bitcast(I32), 0)
         nc.vector.memset(e_scales[:].rearrange("p m c -> p (m c)").bitcast(I32), 0)

@@ -213,7 +213,7 @@ def tile_list_seat_hand_values_kernel(tc, tab_words, tab_scales, offs, wa, wb_wo
             c_bank = product("y_bank" if s == 1 else "c", picked(s), [(c_codes[:, m, :].bitcast(FP8X4), c_scales[:, m, :])
                                                for m in range(PASSES)])
             if s < ADDED_ON_VECTOR:
-                pairs = keep.tile([P, 2, P, 2], BF16, name="pairs", tag=f"pairs{s % 2}", align_bytes=64)
+                pairs = keep.tile([P, 2, P, 2], BF16, name="pairs", tag=f"pairs{s}", align_bytes=64)
                 nc.vector.tensor_tensor(out=pairs[:], in0=by_pair(c_bank), in1=ab[s][:], op=ADD)
                 words = pairs[:].rearrange("j u p e -> j (u p e)").bitcast(F32)
                 h_terms[s] = [words.rearrange("j (u p) -> j u p", u=2)]
@@ -274,8 +274,9 @@ def tile_list_seat_hand_values_kernel(tc, tab_words, tab_scales, offs, wa, wb_wo
         for stage, s in ((features, 0), (features, 1), (quantize_features, 0), (quantize_features, 1)):
             stage(s)
         quantize_weight(raw_d, d_codes, d_scales[:], [(nc.scalar.copy, "rounded_d0"), (nc.scalar.copy, "rounded_d1")])
-        quantize_weight(raw_f, f_codes, f_scales[:], [(nc.vector.tensor_copy, "rounded_f0"), (nc.scalar.copy, "rounded_f1")])
-        for stage, s in ((values, 0), (value_term, 0), (features, 2), (values, 1), (value_term, 1), (quantize_features, 2), (place_values, 0), (features, 3), (quantize_features, 3), (features, 4),):
+        features(2)
+        quantize_weight(raw_f, f_codes, f_scales[:], [(nc.vector.tensor_copy, "ab0"), (nc.scalar.copy, "pairs1")])
+        for stage, s in ((values, 0), (value_term, 0), (values, 1), (value_term, 1), (quantize_features, 2), (features, 3), (features, 4), (place_values, 0), (quantize_features, 3)):
             stage(s)
         for step in range(1, TILES):
             for stage, s in ((feature_product, step + 4), (values, step + 1), (place_values, step), (value_term, step + 1), (feature_sum, step + 4), (quantize_features, step + 3)):

@@ -107,12 +107,12 @@ def tile_list_seat_hand_values_kernel(tc, tab_words, tab_scales, offs, wa, wb_wo
 
         nc.sync.dma_start(out=gather_list[:], in_=offs)
         nc.sync.dma_start(out=scatter_list[:], in_=offs2)
+        nc.sync.dma_start(out=b_codes[:].bitcast(I32), in_=wb_words.rearrange("m p n -> p m n").bitcast(I32))
         for r in range(2):
             nc.sync.dma_start(out=table_scales[r:P:8, :].bitcast(I32),
                               in_=tab_scales[:, r:16:2, :].rearrange("m g c -> g m c").bitcast(I32))
         load_words(0)
         load_scales(nc.sync, bc_scales, 0, wb_scales, range(4))
-        nc.sync.dma_start(out=b_codes[:].bitcast(I32), in_=wb_words.rearrange("m p n -> p m n").bitcast(I32))
         load_words(1)
 
         nc.vector.tensor_copy(out=picked_scales[:], in_=table_scales[:].indirect(gather_list[:]))

@@ -118,7 +118,7 @@ def tile_list_seat_hand_values_kernel(tc, tab_words, tab_scales, offs, wa, wb_wo
         nc.vector.tensor_copy(out=picked_scales[:], in_=table_scales[:].indirect(gather_list[:]))
         picked_words = picked_scales[:].bitcast(I32)
         nc.vector.tensor_copy(out=v_scales[:, 0, :].bitcast(I32), in_=picked_words)
-        for m, odd in ((0, 1), (1, 0), (1, 1)):
+        for m, odd in ((1, 0), (1, 1), (0, 1)):
             for r in range(2):
                 nc.sync.dma_start(out=v_scales[2 * odd + r : P : 32, m, :].bitcast(I32),
                                   in_=picked_words[16 * odd + 8 * m + r : P : 32, :])
@@ -210,7 +210,7 @@ def tile_list_seat_hand_values_kernel(tc, tab_words, tab_scales, offs, wa, wb_wo
                 clear_page(nc.gpsimd, PACK - 1, f"b{s}", 4)
 
         def feature_sum(s):
-            c_bank = product("y_bank" if s == 1 else "c", picked(s), [(c_codes[:, m, :].bitcast(FP8X4), c_scales[:, m, :])
+            c_bank = product({1: "y_bank", 2: "f"}.get(s, "c"), picked(s), [(c_codes[:, m, :].bitcast(FP8X4), c_scales[:, m, :])
                                                for m in range(PASSES)])
             if s < ADDED_ON_VECTOR:
                 pairs = keep.tile([P, 2, P, 2], BF16, name="pairs", tag=f"pairs{s}", align_bytes=64)

from contextlib import ExitStack

import concourse.mybir as mybir
from concourse.masks import make_identity

K, H, N, T, S, T2 = 1024, 512, 512, 2048, 1024, 2048
FLOPS = 2 * S * (3 * K * H + 3 * H * N)

F32 = mybir.dt.float32
BF16 = mybir.dt.bfloat16
I32 = mybir.dt.int32
U32 = mybir.dt.uint32
U16 = mybir.dt.uint16
U8 = mybir.dt.uint8
FP8X4 = mybir.dt.float8_e4m3fn_x4
FP4X4 = mybir.dt.float4_e2m1fn_x4
MULT = mybir.AluOpType.mult
ADD = mybir.AluOpType.add

P = 128
PACK = 4
K_PASS = P * PACK
PASSES = K // K_PASS
TILES = S // P
GATHER = 256
PER_COLUMN = 16
WC_ROW = 8
LEAD = 3
HELD = (1, 1, 1, 7)
ADDED_ON_VECTOR = 5
ON_VECTOR = 1


def interleaved(tile):
    return tile.rearrange("p (c i t) -> p c t i", i=4, t=PACK)


def by_rows(tile):
    return tile.rearrange("p t (c i) -> p c t i", i=4)


def by_slice(bank):
    return bank[:].rearrange("j (p t) -> j t p", t=PACK)


def by_pair(bank):
    return bank[:].rearrange("j (p u e) -> j u p e", u=2, e=2)


def tile_list_seat_hand_values_kernel(tc, tab_words, tab_scales, offs, wa, wb_words, wb_scales, wc_words,
                                                   wc_scales, wd, we_words, we_scales, wf, wgo, offs2, out):
    nc = tc.nc
    with ExitStack() as ctx:
        keep = ctx.enter_context(tc.tile_pool(name="keep", bufs=1))
        ring = ctx.enter_context(tc.tile_pool(name="ring", bufs=2))
        psum = ctx.enter_context(tc.psum_pool(name="psum", bufs=1))

        gather_list = keep.tile([P, S // PER_COLUMN], U16, name="gather_list")
        scatter_list = keep.tile([P, S // PER_COLUMN], U16, name="scatter_list")
        table = [keep.tile([P, T], I32, name=f"table{m}", align_bytes=64) for m in range(PASSES)]
        table_scales = keep.tile([P, T], U8, name="table_scales")
        picked_scales = keep.tile([P, S], U8, name="picked_scales")
        v_scales = keep.tile([P, PASSES, S], U8, name="v_scales", align_bytes=64)
        raw_a = [keep.tile([P, PACK, H], F32, name=f"raw_a{m}") for m in range(PASSES)]
        raw_d = keep.tile([P, PACK, N], F32, name="raw_d")
        raw_f = keep.tile([P, PACK, N], F32, name="raw_f")
        a_codes = [keep.tile([P, H], U32, name=f"a_codes{m}", align_bytes=64) for m in range(PASSES)]
        d_codes = keep.tile([P, N], U32, name="d_codes", align_bytes=64)
        f_codes = keep.tile([P, N], U32, name="f_codes", align_bytes=64)
        b_codes = keep.tile([P, PASSES, 2 * H], U8, name="b_codes", align_bytes=64)
        c_codes = keep.tile([P, PASSES, H], I32, name="c_codes", align_bytes=64)
        e_codes = keep.tile([P, 2 * N], U8, name="e_codes", align_bytes=64)
        bc_scales = keep.tile([P, PASSES, H], U8, name="bc_scales", align_bytes=64)
        c_scales = keep.tile([P, PASSES, H], U8, name="c_scales", align_bytes=64)
        a_scales = keep.tile([P, PASSES, H], U8, name="a_scales", align_bytes=64)
        d_scales = keep.tile([P, N], U8, name="d_scales", align_bytes=64)
        e_scales = keep.tile([P, 1, N], U8, name="e_scales", align_bytes=64)
        f_scales = keep.tile([P, N], U8, name="f_scales", align_bytes=64)
        weights = keep.tile([P, S], F32, name="weights")
        pages = {}
        identity = keep.tile([P, P], F32, name="identity")

        def clear_page(engine, t, tag, pieces=1):
            pages[t] = keep.tile([P, T2], F32, name="page", tag=tag, align_bytes=64)
            for i in range(pieces):
                engine.memset(pages[t][:, i * T2 // pieces : (i + 1) * T2 // pieces].bitcast(I32), 0)

        def load_words(m):
            nc.sync.dma_start(out=table[m][:], in_=tab_words[m].rearrange("p n t -> p (n t)").bitcast(I32))

        def load_rows(raw, rows):
            nc.sync.dma_start(out=raw[:], in_=rows.rearrange("(p t) c -> p t c", t=PACK))

        def load_scales(queue, tile, first, scales, rows):
            for r in rows:
                queue.dma_start(out=tile[first + r : P : 32].bitcast(I32),
                                in_=scales[:, r:16:4, :].rearrange("m q c -> q m c").bitcast(I32))

        nc.gpsimd.memset(table_scales[:].bitcast(I32), 0)
        nc.vector.memset(bc_scales[:].rearrange("p m c -> p (m c)").bitcast(I32), 0)
        nc.vector.memset(c_scales[:].rearrange("p m c -> p (m c)").bitcast(I32), 0)
        nc.vector.memset(e_scales[:].rearrange("p m c -> p (m c)").bitcast(I32), 0)
        nc.vector.memset(v_scales[:, 1, :].bitcast(I32), 0)
        make_identity(nc, identity[:])
        for t in range(2):
            clear_page(nc.vector, t, f"page{t}")

        nc.sync.dma_start(out=gather_list[:], in_=offs)
        nc.sync.dma_start(out=scatter_list[:], in_=offs2)
        nc.sync.dma_start(out=b_codes[:].bitcast(I32), in_=wb_words.rearrange("m p n -> p m n").bitcast(I32))
        for r in range(2):
            nc.sync.dma_start(out=table_scales[r:P:8, :].bitcast(I32),
                              in_=tab_scales[:, r:16:2, :].rearrange("m g c -> g m c").bitcast(I32))
        load_words(0)
        load_scales(nc.sync, bc_scales, 0, wb_scales, range(4))
        load_words(1)

        nc.vector.tensor_copy(out=picked_scales[:], in_=table_scales[:].indirect(gather_list[:]))
        picked_words = picked_scales[:].bitcast(I32)
        nc.vector.tensor_copy(out=v_scales[:, 0, :].bitcast(I32), in_=picked_words)
        for m, odd in ((1, 0), (1, 1), (0, 1)):
            for r in range(2):
                nc.sync.dma_start(out=v_scales[2 * odd + r : P : 32, m, :].bitcast(I32),
                                  in_=picked_words[16 * odd + 8 * m + r : P : 32, :])

        load_rows(raw_a[0], wa[0:K_PASS, :])
        load_scales(nc.sync, c_scales, 0, wc_scales, range(4))
        load_scales(nc.sync, e_scales, 0, we_scales, range(2))
        load_rows(raw_a[1], wa[K_PASS:K, :])
        nc.sync.dma_start(out=c_codes[:], in_=wc_words.rearrange("m p n t -> p m (n t)").bitcast(I32))
        load_rows(raw_d, wd)
        load_rows(raw_f, wf)
        load_scales(nc.sync, e_scales, 0, we_scales, range(2, 4))
        nc.sync.dma_start(out=e_codes[:].bitcast(I32), in_=we_words[0].bitcast(I32))
        nc.sync.dma_start(out=weights[:], in_=wgo)

        v_codes = {}

        def gather_words(m, part):
            v_codes[m, part] = keep.tile([P, GATHER], U32, name=f"v_codes{m}_{part}", align_bytes=64)
            cols = slice(part * GATHER // PER_COLUMN, (part + 1) * GATHER // PER_COLUMN)
            nc.vector.tensor_copy(out=v_codes[m, part][:], in_=table[m][:].bitcast(U32).indirect(gather_list[:, cols]))

        def quantize_weight(raw, codes, scales, shares):
            width = raw.shape[2] // len(shares)
            rounded = []
            for i, (copy, tag) in enumerate(shares):
                tile = keep.tile([P, PACK * width], BF16, name="rounded", tag=tag, align_bytes=64)
                copy(out=interleaved(tile[:]), in_=by_rows(raw[:, :, i * width : (i + 1) * width]))
                rounded.append(tile)
            for i, tile in enumerate(rounded):
                cols = slice(i * width, (i + 1) * width)
                nc.vector.quantize_mx(out=codes[:, cols].bitcast(FP8X4), scales=scales[:, cols], in_=tile[:])

        for part in range(S // GATHER):
            for m in range(PASSES):
                gather_words(m, part)
        for m in range(PASSES):
            quantize_weight(raw_a[m], a_codes[m], a_scales[:, m, :],
                            [(nc.vector.tensor_copy, f"rounded_a{m}{i}") for i in range(2)])

        clear_page(nc.gpsimd, 2, "rounded_a11", 4)

        def product(tag, lhs, rhs):
            bank = psum.tile([P, K_PASS], F32, name="bank", tag=tag)
            for m, ((codes, scales), (w_codes, w_scales)) in enumerate(zip(lhs, rhs)):
                nc.tensor.matmul_mx(out=bank[:], lhsT=codes, lhsT_scale=scales, rhs=w_codes, rhs_scale=w_scales,
                                    start=(m == 0), stop=(m == len(lhs) - 1))
            return bank

        def copied(tag, view):
            tile = keep.tile(view.shape, F32, name="copied", tag=tag, align_bytes=64)
            nc.scalar.copy(out=tile[:], in_=view)
            return tile

        def times(tag, view, factor):
            tile = keep.tile(view.shape, F32, name="times", tag=tag, align_bytes=64)
            nc.vector.tensor_tensor(out=tile[:], in0=view, in1=factor[:], op=MULT)
            return tile

        def turned_sum(name, terms):
            bank = psum.tile([P, PACK, P], F32, name="bank", tag=name)
            slices = terms[0].shape[1]
            for i, term in enumerate(terms):
                for t in range(slices):
                    nc.tensor.matmul(out=bank[:, t, :], lhsT=term[:, t, :], rhs=identity[:], is_transpose=True,
                                     start=(i == 0 and t == 0), stop=(i == len(terms) - 1 and t == slices - 1))
            return bank

        b, ab, h_terms, h, y_terms = {}, {}, {}, {}, {}

        def picked(s):
            part, first = divmod(s * P, GATHER)
            return [(v_codes[m, part][:, first : first + P].bitcast(FP8X4), v_scales[:, m, s * P : (s + 1) * P])
                    for m in range(PASSES)]

        def order(s):
            return by_pair if s < ADDED_ON_VECTOR else by_slice

        def feature_factor(s):
            b_bank = product("cedf"[s % 4], picked(s), [(b_codes[:, m, :].bitcast(FP4X4), bc_scales[:, m, :])
                                               for m in range(PASSES)])
            b[s] = copied(f"b{s}", order(s)(b_bank))

        def feature_product(s):
            a_bank = product(f"a{s % 2}", picked(s), [(a_codes[m][:].bitcast(FP8X4), a_scales[:, m, :])
                                              for m in range(PASSES)])
            ab[s] = times(f"ab{s % 2}", order(s)(a_bank), b[s])
            if s == TILES - 1:
                clear_page(nc.gpsimd, PACK - 1, f"b{s}", 4)

        def feature_sum(s):
            c_bank = product({1: "y_bank", 2: "f"}.get(s, "c"), picked(s), [(c_codes[:, m, :].bitcast(FP8X4), c_scales[:, m, :])
                                               for m in range(PASSES)])
            if s < ADDED_ON_VECTOR:
                pairs = keep.tile([P, 2, P, 2], BF16, name="pairs", tag=f"pairs{s}", align_bytes=64)
                nc.vector.tensor_tensor(out=pairs[:], in0=by_pair(c_bank), in1=ab[s][:], op=ADD)
                words = pairs[:].rearrange("j u p e -> j (u p e)").bitcast(F32)
                h_terms[s] = [words.rearrange("j (u p) -> j u p", u=2)]
            else:
                h_terms[s] = [copied(f"c{s % 2}", by_slice(c_bank))[:], ab[s][:]]

        def features(s):
            feature_product(s)
            feature_sum(s)

        def quantize_features(s):
            bank = turned_sum("h_bank", h_terms[s])
            rounded = ring.tile([P, P * PACK], BF16, name="h_rounded", align_bytes=64)
            if s < ADDED_ON_VECTOR:
                nc.scalar.copy(out=rounded[:].bitcast(F32).rearrange("p (j u) -> p j u", u=2),
                               in_=bank[:, 0:2, :].rearrange("p u j -> p j u"))
            else:
                nc.scalar.copy(out=rounded[:].rearrange("p (j t) -> p j t", t=PACK),
                               in_=bank[:].rearrange("p t j -> p j t"))
            codes = keep.tile([P, P], U32, name=f"h_codes{s}", align_bytes=64)
            scales = keep.tile([P, P], U8, name=f"h_scales{s}", align_bytes=64)
            nc.vector.quantize_mx(out=codes[:].bitcast(FP8X4), scales=scales[:], in_=rounded[:])
            h[s] = [(codes[:].bitcast(FP8X4), scales[:])]

        def values(s):
            e = copied(f"e{s % 2}", by_slice(product("e", h[s], [(e_codes[:].bitcast(FP4X4), e_scales[:, 0, :])])))
            de = times(f"de{s % 3}", by_slice(product("d", h[s], [(d_codes[:].bitcast(FP8X4), d_scales[:])])), e)
            y_terms[s] = [de[:]]

        def value_term(s):
            f = copied(f"f{s % 3}", by_slice(product("f", h[s], [(f_codes[:].bitcast(FP8X4), f_scales[:])])))
            y_terms[s] = [f[:]] + y_terms[s]

        y = keep.tile([P, PACK, S], F32, name="y")

        def scatter(t, lo, hi):
            window = pages[t][:].indirect(scatter_list[:, lo // PER_COLUMN : hi // PER_COLUMN])
            nc.vector.tensor_tensor(out=window, in0=y[:, t, lo:hi], in1=weights[:, lo:hi], op=MULT)
            if hi == S:
                nc.sync.dma_start(out=out.rearrange("(p t) c -> p t c", t=PACK)[:, t, :], in_=pages[t][:])

        def place_values(s):
            first = 1 if s == 0 or s >= 4 else 0
            if first:
                bank = turned_sum("a0" if s else "e", [term[:, :first] for term in y_terms[s]])
                nc.scalar.copy(out=y[:, :first, s * P : (s + 1) * P], in_=bank[:, :first])
            bank = turned_sum("y_bank", [term[:, first:] for term in y_terms[s]])
            nc.scalar.copy(out=y[:, first:, s * P : (s + 1) * P], in_=bank[:, : PACK - first])
            for t in range(PACK - 1):
                scatter(t, s * P, (s + 1) * P)
            if s == 3:
                scatter(PACK - 1, 0, 1 * P)
            if s == TILES - 1:
                scatter(PACK - 1, 1 * P, S)

        for s in range(TILES):
            feature_factor(s)
        for stage, s in ((features, 0), (features, 1), (quantize_features, 0), (quantize_features, 1)):
            stage(s)
        quantize_weight(raw_d, d_codes, d_scales[:], [(nc.scalar.copy, "rounded_d0"), (nc.scalar.copy, "rounded_d1")])
        features(2)
        quantize_weight(raw_f, f_codes, f_scales[:], [(nc.vector.tensor_copy, "ab0"), (nc.scalar.copy, "pairs1")])
        for stage, s in ((values, 0), (value_term, 0), (values, 1), (value_term, 1), (quantize_features, 2), (features, 3), (features, 4), (place_values, 0), (quantize_features, 3)):
            stage(s)
        for step in range(1, TILES):
            for stage, s in ((feature_product, step + 4), (values, step + 1), (place_values, step), (value_term, step + 1), (feature_sum, step + 4), (quantize_features, step + 3)):
                if s < TILES:
                    stage(s)
